import numpy as np
import ml_dtypes


def mxq(x, axis, fmt="e4m3"):
    dtype, down = {"e4m3": (ml_dtypes.float8_e4m3fn, 7), "e5m2": (ml_dtypes.float8_e5m2, 14)}[fmt]
    v = np.moveaxis(np.asarray(x, np.float32).astype(ml_dtypes.bfloat16).astype(np.float64), axis, -1)
    blocks = v.reshape(v.shape[:-1] + (-1, 32))
    amax = np.abs(blocks).max(-1, keepdims=True)
    byte = np.maximum(np.where(amax > 0, np.frexp(amax)[1] - 1 + 127, 0) - down, 1)
    scale = np.exp2(byte - 127.0)
    codes = (blocks / scale).astype(np.float32).astype(dtype).astype(np.float64)
    return np.moveaxis((codes * scale).reshape(v.shape), -1, axis)


WIDE = False


def mx_kscale(k):
    if not WIDE:
        return np.ones(k)
    levels = np.array([10, -10, 5, -5, 0])
    if k % 512:
        return np.exp2(np.random.permutation(np.resize(levels, k // 32))).repeat(32)
    a = np.empty((k // 512, 16))
    for p in range(k // 512):
        a[p, :8] = np.random.permutation(np.resize(levels, 8))
        for g in range(8):
            far = levels[np.abs(levels - a[p, g]) >= 10]
            a[p, g + 8] = far[np.random.randint(len(far))]
    return np.exp2(a.ravel()).repeat(32)


def f64(x):
    return np.asarray(x).astype(np.float64)


def striped(idx):
    return np.tile(idx.reshape(-1, 16).T, (8, 1)).astype(np.uint16)


def unstriped(offs):
    return offs[:16].T.reshape(-1).astype(np.int64)


def striped8(idx):
    return np.concatenate([x.reshape(-1, 16).T for x in idx]).astype(np.uint16)


def runs(offs, k):
    lists = np.stack([offs[16 * r : 16 * r + 16].T.reshape(-1) for r in range(8)]).astype(np.int64)
    return lists[np.arange(k) % 512 // 64]


def pack_weight(w):
    k, n = w.shape
    w = f64(np.asarray(w, np.float32).astype(ml_dtypes.bfloat16)).reshape(k // 32, 32, n)
    amax = np.abs(w).max(1)
    byte = np.clip(np.where(amax > 0, np.frexp(amax)[1] - 1 + 127 - 7, 1), 1, 254)
    scaled = (w * np.exp2(127.0 - byte)[:, None, :]).reshape(k, n).astype(np.float32)
    words = np.ascontiguousarray(scaled.reshape(k // 512, 128, 4, n).transpose(0, 1, 3, 2)).astype(ml_dtypes.float8_e4m3fn).view(np.uint8)
    return words, np.ascontiguousarray(byte.astype(np.uint8).reshape(k // 512, 16, n))


def unpack_weight(words, scales):
    g, p, n, _ = words.shape
    vals = np.ascontiguousarray(words).view(ml_dtypes.float8_e4m3fn).astype(np.float64) * np.repeat(np.exp2(scales.astype(np.float64) - 127.0), 8, axis=1)[..., None]
    return vals.transpose(0, 1, 3, 2).reshape(g * 512, n)


K, T, S, N, U = 512, 2048, 512, 512, 1024


def setup_inputs():
    n = np.random.standard_normal
    s = mx_kscale(K)[:, None]
    packed_xT = pack_weight(n((K, T)) * s)
    return {
        "x_words": packed_xT[0],
        "x_scales": packed_xT[1],
        "w1": (n((K, N)) / np.sqrt(K) / s).astype(np.float32),
        "old": n((N, U)).astype(np.float32),
        "adv": n((N, U)).astype(np.float32),
        "offs": striped(np.random.permutation(T)[:S]),
        "st": striped8(np.stack([np.random.permutation(U)[:S] for _ in range(8)])),
    }


def reference(x_words, x_scales, w1, old, adv, offs, st):
    xq = unpack_weight(x_words, x_scales)[:, unstriped(offs)]
    y = mxq(f64(w1), 0, "e4m3").T @ xq
    rt = np.exp(0.25 * (y - (f64(old)[np.arange(N)[:, None], runs(st, N)])))
    a = f64(adv)[np.arange(N)[:, None], runs(st, N)]
    return np.minimum(rt * a, np.clip(rt, 0.8, 1.25) * a)

@@ -1,0 +1,173 @@
+from contextlib import ExitStack
+
+import concourse.mybir as mybir
+from concourse.masks import make_identity
+
+K, T, S, N, U = 512, 2048, 512, 512, 1024
+FLOPS = 2 * K * N * S
+
+F32 = mybir.dt.float32
+BF16 = mybir.dt.bfloat16
+I32 = mybir.dt.int32
+U32 = mybir.dt.uint32
+U16 = mybir.dt.uint16
+U8 = mybir.dt.uint8
+FP8X4 = mybir.dt.float8_e4m3fn_x4
+ACT = mybir.ActivationFunctionType
+ALU = mybir.AluOpType
+
+P = 128
+PACK = 4
+TILES = N // P
+HALVES = 2
+LOW, HIGH = 0.8, 1.25
+
+
+def tile_picked_ppo8_none_p_kernel(tc, x_words, x_scales, w1, old, adv, offs, st, out):
+    nc = tc.nc
+    with ExitStack() as ctx:
+        keep = ctx.enter_context(tc.tile_pool(name="keep", bufs=1))
+        work = ctx.enter_context(tc.tile_pool(name="work", bufs=2))
+        psum_y = ctx.enter_context(tc.psum_pool(name="psum_y", bufs=2))
+        psum_t = ctx.enter_context(tc.psum_pool(name="psum_t", bufs=2))
+        psum_c = ctx.enter_context(tc.psum_pool(name="psum_c", bufs=4))
+
+        offs_sb = keep.tile([P, S // 16], U16, name="offs_sb")
+        st_sb = keep.tile([P, S // 16], U16, name="st_sb")
+        nc.sync.dma_start(offs_sb[:], offs)
+        nc.sync.dma_start(st_sb[:], st)
+
+        scale_table = keep.tile([P, T], U8, name="scale_table")
+        nc.gpsimd.memset(scale_table[:].bitcast(I32), 0)
+        scale_rows = keep.tile([P, T // 4], I32, name="scale_rows")
+        for q in range(4):
+            nc.sync.dma_start(scale_rows[32 * q : 32 * q + 4, :], x_scales[0, 4 * q : 4 * q + 4, :].bitcast(I32))
+        for q in range(4):
+            rows = slice(32 * q, 32 * q + 4)
+            nc.vector.tensor_copy(scale_table[rows, :].bitcast(I32), scale_rows[rows, :])
+
+        warm = keep.tile([P, 1], F32, name="warm")
+        nc.vector.memset(warm[:], 0.0)
+        warm_out = keep.tile([P, 1], F32, name="warm_out")
+        nc.scalar.activation(warm_out[:], warm[:], ACT.Exp)
+
+        w_rows = w1.rearrange("(p j) c -> p j c", j=PACK)
+        half = N // HALVES
+        w_raw = []
+        for h in range(HALVES):
+            piece = keep.tile([P, PACK, half], F32, name=f"w_raw{h}")
+            nc.sync.dma_start(piece[:], w_rows[:, :, h * half : (h + 1) * half])
+            w_raw.append(piece)
+        word_table = keep.tile([P, T], I32, name="word_table")
+        nc.sync.dma_start(word_table[:], x_words[0].rearrange("p n r -> p (n r)").bitcast(I32))
+
+        old_rows = old.rearrange("(p t) u -> p t u", t=TILES)
+        adv_rows = adv.rearrange("(p t) u -> p t u", t=TILES)
+        out_rows = out.rearrange("(p t) s -> p t s", t=TILES)
+        old_sb, adv_sb = {}, {}
+
+        def load_adv(t):
+            adv_sb[t] = keep.tile([P, U], F32, name=f"adv{t}", tag=f"adv{t}")
+            nc.sync.dma_start(adv_sb[t][:], adv_rows[:, t, :])
+
+        def load_old(t):
+            old_sb[t] = keep.tile([P, U], F32, name=f"old{t}", tag=f"old{t}")
+            nc.sync.dma_start(old_sb[t][:], old_rows[:, t, :])
+
+        load_adv(0)
+        load_adv(1)
+        load_old(0)
+        for t in range(1, TILES):
+            load_old(t)
+            if t + 1 < TILES:
+                load_adv(t + 1)
+
+        ident = keep.tile([P, P], F32, name="ident")
+        make_identity(nc, ident[:])
+
+        x_scale = keep.tile([P, S], U8, name="x_scale", align_bytes=64)
+        nc.vector.tensor_copy(x_scale[:], scale_table[:].indirect(offs_sb[:]))
+
+        grouped = keep.tile([P, TILES, P, PACK], BF16, name="grouped", align_bytes=64)
+        mh = P // HALVES
+        for h in range(HALVES):
+            dst = grouped[:, :, h * mh : (h + 1) * mh, :].rearrange("p t m j -> p m j t")
+            src = w_raw[h][:].rearrange("p j (m t) -> p m j t", t=TILES)
+            if h == 0:
+                nc.scalar.copy(dst, src)
+            else:
+                nc.vector.tensor_copy(dst, src)
+        w_code = keep.tile([P, N], U32, name="w_code", align_bytes=64)
+        w_scale = keep.tile([P, N], U8, name="w_scale", align_bytes=64)
+        nc.vector.quantize_mx(w_code[:].bitcast(FP8X4), w_scale[:], grouped[:].rearrange("p t m j -> p (t m j)"))
+
+        x_code = keep.tile([P, S], U32, name="x_code", align_bytes=64)
+        nc.vector.tensor_copy(x_code[:], word_table[:].bitcast(U32).indirect(offs_sb[:]))
+
+        y_sb, a_sb, cap, ratio, plain = {}, {}, {}, {}, {}
+
+        def project(t):
+            y_ps = psum_y.tile([P, S], F32, name="y_ps")
+            cols = slice(t * P, (t + 1) * P)
+            nc.tensor.matmul_mx(
+                y_ps[:],
+                lhsT=w_code[:, cols].bitcast(FP8X4),
+                lhsT_scale=w_scale[:, cols],
+                rhs=x_code[:].bitcast(FP8X4),
+                rhs_scale=x_scale[:],
+                start=True,
+                stop=True,
+            )
+            y_sb[t] = work.tile([P, S], F32, name="y_sb")
+            nc.scalar.copy(y_sb[t][:], y_ps[:])
+
+        def fetch_adv(t):
+            a_sb[t] = keep.tile([P, S], F32, name=f"a{t}")
+            nc.vector.tensor_copy(a_sb[t][:], adv_sb[t][:].indirect(st_sb[:]))
+
+        def bound(t):
+            turned = psum_t.tile([P, S], F32, name="turned")
+            for b in range(S // P):
+                blk = slice(b * P, (b + 1) * P)
+                nc.tensor.transpose(turned[:, blk], a_sb[t][:, blk], ident[:])
+            base = keep.tile([P, S], F32, name=f"base{t}", tag=f"diff{t - 1}")
+            extra = work.tile([P, S], F32, name="extra")
+            nc.scalar.activation(base[:], turned[:], ACT.Copy, scale=LOW)
+            nc.scalar.activation(extra[:], turned[:], ACT.Relu, scale=HIGH - LOW)
+            cap[t] = psum_c.tile([P, S], F32, name="cap")
+            for b in range(S // P):
+                blk = slice(b * P, (b + 1) * P)
+                nc.tensor.matmul(cap[t][:, blk], base[:, blk], ident[:], start=True, stop=False, is_transpose=True)
+                nc.tensor.matmul(cap[t][:, blk], extra[:, blk], ident[:], start=False, stop=True, is_transpose=True)
+
+        def fetch_old(t):
+            diff = keep.tile([P, S], F32, name=f"diff{t}", tag=f"diff{t}")
+            nc.vector.tensor_tensor(diff[:], old_sb[t][:].indirect(st_sb[:]), y_sb[t][:], ALU.subtract)
+            ratio[t] = keep.tile([P, S], F32, name=f"ratio{t}")
+            nc.scalar.activation(ratio[t][:], diff[:], ACT.Exp, scale=-0.25)
+
+        def multiply(t):
+            plain[t] = keep.tile([P, S], F32, name=f"plain{t}")
+            nc.vector.tensor_tensor(plain[t][:], ratio[t][:], a_sb[t][:], ALU.mult)
+
+        def finish(t):
+            result = keep.tile([P, S], F32, name=f"result{t}")
+            nc.vector.tensor_tensor(result[:], plain[t][:], cap[t][:], ALU.min)
+            nc.sync.dma_start(out_rows[:, t, :], result[:])
+
+        project(0)
+        fetch_adv(0)
+        project(1)
+        fetch_adv(1)
+        bound(0)
+        fetch_old(0)
+        for t in range(TILES):
+            if t + 2 < TILES:
+                project(t + 2)
+            if t + 1 < TILES:
+                bound(t + 1)
+                fetch_old(t + 1)
+            multiply(t)
+            if t + 2 < TILES:
+                fetch_adv(t + 2)
+            finish(t)

@@ -51,15 +51,6 @@ def tile_picked_ppo8_none_p_kernel(tc, x_words, x_scales, w1, old, adv, offs, st
         warm_out = keep.tile([P, 1], F32, name="warm_out")
         nc.scalar.activation(warm_out[:], warm[:], ACT.Exp)
 
-        w_rows = w1.rearrange("(p j) c -> p j c", j=PACK)
-        half = N // HALVES
-        w_raw = []
-        for h in range(HALVES):
-            piece = keep.tile([P, PACK, half], F32, name=f"w_raw{h}")
-            nc.sync.dma_start(piece[:], w_rows[:, :, h * half : (h + 1) * half])
-            w_raw.append(piece)
-        word_table = keep.tile([P, T], I32, name="word_table")
-        nc.sync.dma_start(word_table[:], x_words[0].rearrange("p n r -> p (n r)").bitcast(I32))
 
         old_rows = old.rearrange("(p t) u -> p t u", t=TILES)
         adv_rows = adv.rearrange("(p t) u -> p t u", t=TILES)
@@ -74,35 +65,25 @@ def tile_picked_ppo8_none_p_kernel(tc, x_words, x_scales, w1, old, adv, offs, st
             old_sb[t] = keep.tile([P, U], F32, name=f"old{t}", tag=f"old{t}")
             nc.sync.dma_start(old_sb[t][:], old_rows[:, t, :])
 
-        load_adv(0)
-        load_adv(1)
-        load_old(0)
-        for t in range(1, TILES):
+        for t in range(2):
+            load_adv(t)
+        w_rows = w1.rearrange("(p j) c -> p j c", j=PACK)
+        half = N // HALVES
+        w_raw = []
+        for h in range(HALVES):
+            piece = keep.tile([P, PACK, half], F32, name=f"w_raw{h}", tag=f"w_raw{h}")
+            nc.sync.dma_start(piece[:], w_rows[:, :, h * half : (h + 1) * half])
+            w_raw.append(piece)
+        word_table = keep.tile([P, T], I32, name="word_table")
+        nc.sync.dma_start(word_table[:], x_words[0].rearrange("p n r -> p (n r)").bitcast(I32))
+        for t in range(2, TILES):
+            load_adv(t)
+        for t in range(TILES):
             load_old(t)
-            if t + 1 < TILES:
-                load_adv(t + 1)
 
         ident = keep.tile([P, P], F32, name="ident")
         make_identity(nc, ident[:])
 
-        x_scale = keep.tile([P, S], U8, name="x_scale", align_bytes=64)
-        nc.vector.tensor_copy(x_scale[:], scale_table[:].indirect(offs_sb[:]))
-
-        grouped = keep.tile([P, TILES, P, PACK], BF16, name="grouped", align_bytes=64)
-        mh = P // HALVES
-        for h in range(HALVES):
-            dst = grouped[:, :, h * mh : (h + 1) * mh, :].rearrange("p t m j -> p m j t")
-            src = w_raw[h][:].rearrange("p j (m t) -> p m j t", t=TILES)
-            if h == 0:
-                nc.scalar.copy(dst, src)
-            else:
-                nc.vector.tensor_copy(dst, src)
-        w_code = keep.tile([P, N], U32, name="w_code", align_bytes=64)
-        w_scale = keep.tile([P, N], U8, name="w_scale", align_bytes=64)
-        nc.vector.quantize_mx(w_code[:].bitcast(FP8X4), w_scale[:], grouped[:].rearrange("p t m j -> p (t m j)"))
-
-        x_code = keep.tile([P, S], U32, name="x_code", align_bytes=64)
-        nc.vector.tensor_copy(x_code[:], word_table[:].bitcast(U32).indirect(offs_sb[:]))
 
         y_sb, a_sb, cap, ratio, plain = {}, {}, {}, {}, {}
 
@@ -130,10 +111,10 @@ def tile_picked_ppo8_none_p_kernel(tc, x_words, x_scales, w1, old, adv, offs, st
             for b in range(S // P):
                 blk = slice(b * P, (b + 1) * P)
                 nc.tensor.transpose(turned[:, blk], a_sb[t][:, blk], ident[:])
-            base = keep.tile([P, S], F32, name=f"base{t}", tag=f"diff{t - 1}")
-            extra = work.tile([P, S], F32, name="extra")
-            nc.scalar.activation(base[:], turned[:], ACT.Copy, scale=LOW)
-            nc.scalar.activation(extra[:], turned[:], ACT.Relu, scale=HIGH - LOW)
+            parts = keep.tile([P, 2 * S], F32, name=f"parts{t}", tag="w_raw0")
+            base, extra = parts[:, :S], parts[:, S:]
+            nc.scalar.activation(base, turned[:], ACT.Copy, scale=LOW)
+            nc.scalar.activation(extra, turned[:], ACT.Relu, scale=HIGH - LOW)
             cap[t] = psum_c.tile([P, S], F32, name="cap")
             for b in range(S // P):
                 blk = slice(b * P, (b + 1) * P)
@@ -155,19 +136,46 @@ def tile_picked_ppo8_none_p_kernel(tc, x_words, x_scales, w1, old, adv, offs, st
             nc.vector.tensor_tensor(result[:], plain[t][:], cap[t][:], ALU.min)
             nc.sync.dma_start(out_rows[:, t, :], result[:])
 
-        project(0)
         fetch_adv(0)
-        project(1)
         fetch_adv(1)
+        x_scale = keep.tile([P, S], U8, name="x_scale", align_bytes=64)
+        nc.vector.tensor_copy(x_scale[:], scale_table[:].indirect(offs_sb[:]))
+
+        grouped = keep.tile([P, TILES, P, PACK], BF16, name="grouped", align_bytes=64)
+        mh = P // HALVES
+        for h in range(HALVES):
+            dst = grouped[:, :, h * mh : (h + 1) * mh, :].rearrange("p t m j -> p m j t")
+            src = w_raw[h][:].rearrange("p j (m t) -> p m j t", t=TILES)
+            if h == 0:
+                nc.scalar.copy(dst, src)
+            else:
+                nc.vector.tensor_copy(dst, src)
+        w_code = keep.tile([P, N], U32, name="w_code", align_bytes=64)
+        w_scale = keep.tile([P, N], U8, name="w_scale", align_bytes=64)
+        nc.vector.quantize_mx(w_code[:].bitcast(FP8X4), w_scale[:], grouped[:].rearrange("p t m j -> p (t m j)"))
+
+        x_code = keep.tile([P, S], U32, name="x_code", align_bytes=64)
+        nc.vector.tensor_copy(x_code[:], word_table[:].bitcast(U32).indirect(offs_sb[:]))
         bound(0)
+        bound(1)
+
+        project(0)
+        project(1)
+        fetch_adv(2)
+        fetch_adv(3)
+        bound(2)
         fetch_old(0)
-        for t in range(TILES):
-            if t + 2 < TILES:
-                project(t + 2)
-            if t + 1 < TILES:
-                bound(t + 1)
-                fetch_old(t + 1)
-            multiply(t)
-            if t + 2 < TILES:
-                fetch_adv(t + 2)
-            finish(t)
+        project(2)
+        fetch_old(1)
+        bound(3)
+        project(3)
+        multiply(0)
+        fetch_old(2)
+        finish(0)
+        multiply(1)
+        fetch_old(3)
+        finish(1)
+        multiply(2)
+        multiply(3)
+        finish(2)
+        finish(3)

@@ -39,12 +39,6 @@ def tile_picked_ppo8_none_p_kernel(tc, x_words, x_scales, w1, old, adv, offs, st
 
         scale_table = keep.tile([P, T], U8, name="scale_table")
         nc.gpsimd.memset(scale_table[:].bitcast(I32), 0)
-        scale_rows = keep.tile([P, T // 4], I32, name="scale_rows")
-        for q in range(4):
-            nc.sync.dma_start(scale_rows[32 * q : 32 * q + 4, :], x_scales[0, 4 * q : 4 * q + 4, :].bitcast(I32))
-        for q in range(4):
-            rows = slice(32 * q, 32 * q + 4)
-            nc.vector.tensor_copy(scale_table[rows, :].bitcast(I32), scale_rows[rows, :])
 
         warm = keep.tile([P, 1], F32, name="warm")
         nc.vector.memset(warm[:], 0.0)
@@ -65,15 +59,15 @@ def tile_picked_ppo8_none_p_kernel(tc, x_words, x_scales, w1, old, adv, offs, st
             old_sb[t] = keep.tile([P, U], F32, name=f"old{t}", tag=f"old{t}")
             nc.sync.dma_start(old_sb[t][:], old_rows[:, t, :])
 
-        for t in range(2):
-            load_adv(t)
+        load_adv(0)
+        for q in range(4):
+            nc.sync.dma_start(
+                scale_table[32 * q : 32 * q + 4, :].bitcast(I32), x_scales[0, 4 * q : 4 * q + 4, :].bitcast(I32)
+            )
         w_rows = w1.rearrange("(p j) c -> p j c", j=PACK)
-        half = N // HALVES
-        w_raw = []
-        for h in range(HALVES):
-            piece = keep.tile([P, PACK, half], F32, name=f"w_raw{h}", tag=f"w_raw{h}")
-            nc.sync.dma_start(piece[:], w_rows[:, :, h * half : (h + 1) * half])
-            w_raw.append(piece)
+        w_raw = keep.tile([P, PACK, N], F32, name="w_raw", tag="w_raw0")
+        nc.sync.dma_start(w_raw[:], w_rows)
+        load_adv(1)
         word_table = keep.tile([P, T], I32, name="word_table")
         nc.sync.dma_start(word_table[:], x_words[0].rearrange("p n r -> p (n r)").bitcast(I32))
         for t in range(2, TILES):
@@ -89,11 +83,12 @@ def tile_picked_ppo8_none_p_kernel(tc, x_words, x_scales, w1, old, adv, offs, st
 
         def project(t):
             y_ps = psum_y.tile([P, S], F32, name="y_ps")
-            cols = slice(t * P, (t + 1) * P)
+            h, i = divmod(t, TILES // HALVES)
+            cols = slice(i * P, (i + 1) * P)
             nc.tensor.matmul_mx(
                 y_ps[:],
-                lhsT=w_code[:, cols].bitcast(FP8X4),
-                lhsT_scale=w_scale[:, cols],
+                lhsT=w_code[h][:, cols].bitcast(FP8X4),
+                lhsT_scale=w_scale[h][:, cols],
                 rhs=x_code[:].bitcast(FP8X4),
                 rhs_scale=x_scale[:],
                 start=True,
@@ -141,18 +136,22 @@ def tile_picked_ppo8_none_p_kernel(tc, x_words, x_scales, w1, old, adv, offs, st
         x_scale = keep.tile([P, S], U8, name="x_scale", align_bytes=64)
         nc.vector.tensor_copy(x_scale[:], scale_table[:].indirect(offs_sb[:]))
 
-        grouped = keep.tile([P, TILES, P, PACK], BF16, name="grouped", align_bytes=64)
-        mh = P // HALVES
+        w_code, w_scale = [], []
+        per_half = TILES // HALVES
+        w_cols = w_raw[:].rearrange("p j (m t) -> p m t j", t=TILES)
         for h in range(HALVES):
-            dst = grouped[:, :, h * mh : (h + 1) * mh, :].rearrange("p t m j -> p m j t")
-            src = w_raw[h][:].rearrange("p j (m t) -> p m j t", t=TILES)
+            grouped = keep.tile([P, per_half, P, PACK], BF16, name=f"grouped{h}", align_bytes=64)
+            dst = grouped[:].rearrange("p t m j -> p m t j")
+            src = w_cols[:, :, h * per_half : (h + 1) * per_half, :]
             if h == 0:
-                nc.scalar.copy(dst, src)
-            else:
                 nc.vector.tensor_copy(dst, src)
-        w_code = keep.tile([P, N], U32, name="w_code", align_bytes=64)
-        w_scale = keep.tile([P, N], U8, name="w_scale", align_bytes=64)
-        nc.vector.quantize_mx(w_code[:].bitcast(FP8X4), w_scale[:], grouped[:].rearrange("p t m j -> p (t m j)"))
+            else:
+                nc.scalar.copy(dst, src)
+            codes = keep.tile([P, per_half * P], U32, name=f"w_code{h}", align_bytes=64)
+            scales = keep.tile([P, per_half * P], U8, name=f"w_scale{h}", align_bytes=64)
+            nc.vector.quantize_mx(codes[:].bitcast(FP8X4), scales[:], grouped[:].rearrange("p t m j -> p (t m j)"))
+            w_code.append(codes)
+            w_scale.append(scales)
 
         x_code = keep.tile([P, S], U32, name="x_code", align_bytes=64)
         nc.vector.tensor_copy(x_code[:], word_table[:].bitcast(U32).indirect(offs_sb[:]))

@@ -18,19 +18,21 @@ ALU = mybir.AluOpType
 
 P = 128
 PACK = 4
+QUADRANTS = 4
 TILES = N // P
-HALVES = 2
+PAIR = 2
 LOW, HIGH = 0.8, 1.25
+Y_BUFFERS = 3
 
 
 def tile_picked_ppo8_none_p_kernel(tc, x_words, x_scales, w1, old, adv, offs, st, out):
     nc = tc.nc
     with ExitStack() as ctx:
         keep = ctx.enter_context(tc.tile_pool(name="keep", bufs=1))
-        work = ctx.enter_context(tc.tile_pool(name="work", bufs=2))
+        y_pool = ctx.enter_context(tc.tile_pool(name="y_pool", bufs=Y_BUFFERS))
         psum_y = ctx.enter_context(tc.psum_pool(name="psum_y", bufs=2))
-        psum_t = ctx.enter_context(tc.psum_pool(name="psum_t", bufs=2))
-        psum_c = ctx.enter_context(tc.psum_pool(name="psum_c", bufs=4))
+        psum_turned = ctx.enter_context(tc.psum_pool(name="psum_turned", bufs=2))
+        psum_cap = ctx.enter_context(tc.psum_pool(name="psum_cap", bufs=TILES))
 
         offs_sb = keep.tile([P, S // 16], U16, name="offs_sb")
         st_sb = keep.tile([P, S // 16], U16, name="st_sb")
@@ -39,86 +41,82 @@ def tile_picked_ppo8_none_p_kernel(tc, x_words, x_scales, w1, old, adv, offs, st
 
         scale_table = keep.tile([P, T], U8, name="scale_table")
         nc.gpsimd.memset(scale_table[:].bitcast(I32), 0)
-
-        warm = keep.tile([P, 1], F32, name="warm")
-        nc.vector.memset(warm[:], 0.0)
-        warm_out = keep.tile([P, 1], F32, name="warm_out")
-        nc.scalar.activation(warm_out[:], warm[:], ACT.Exp)
-
+        scale_rows = keep.tile([P, T // 4], I32, name="scale_rows")
+        for q in range(QUADRANTS):
+            nc.sync.dma_start(scale_rows[32 * q : 32 * q + 4, :], x_scales[0, 4 * q : 4 * q + 4, :].bitcast(I32))
+        for q in range(QUADRANTS):
+            live = slice(32 * q, 32 * q + 4)
+            nc.vector.tensor_copy(scale_table[live, :].bitcast(I32), scale_rows[live, :])
 
         old_rows = old.rearrange("(p t) u -> p t u", t=TILES)
         adv_rows = adv.rearrange("(p t) u -> p t u", t=TILES)
         out_rows = out.rearrange("(p t) s -> p t s", t=TILES)
-        old_sb, adv_sb = {}, {}
 
-        def load_adv(t):
-            adv_sb[t] = keep.tile([P, U], F32, name=f"adv{t}", tag=f"adv{t}")
-            nc.sync.dma_start(adv_sb[t][:], adv_rows[:, t, :])
+        def load_table(rows, t, name):
+            table = keep.tile([P, U], F32, name=name)
+            nc.sync.dma_start(table[:], rows[:, t, :])
+            return table
 
-        def load_old(t):
-            old_sb[t] = keep.tile([P, U], F32, name=f"old{t}", tag=f"old{t}")
-            nc.sync.dma_start(old_sb[t][:], old_rows[:, t, :])
-
-        load_adv(0)
-        for q in range(4):
-            nc.sync.dma_start(
-                scale_table[32 * q : 32 * q + 4, :].bitcast(I32), x_scales[0, 4 * q : 4 * q + 4, :].bitcast(I32)
-            )
-        w_rows = w1.rearrange("(p j) c -> p j c", j=PACK)
-        w_raw = keep.tile([P, PACK, N], F32, name="w_raw", tag="w_raw0")
-        nc.sync.dma_start(w_raw[:], w_rows)
-        load_adv(1)
+        adv_table = [load_table(adv_rows, 0, "adv0")]
+        w_raw = keep.tile([P, PACK, N], F32, name="w_raw", tag="w_raw")
+        nc.sync.dma_start(w_raw[:], w1.rearrange("(p j) m -> p j m", j=PACK))
         word_table = keep.tile([P, T], I32, name="word_table")
         nc.sync.dma_start(word_table[:], x_words[0].rearrange("p n r -> p (n r)").bitcast(I32))
-        for t in range(2, TILES):
-            load_adv(t)
-        for t in range(TILES):
-            load_old(t)
+        adv_table.extend(load_table(adv_rows, t, f"adv{t}") for t in range(1, TILES))
+        old_table = [load_table(old_rows, t, f"old{t}") for t in range(TILES)]
 
         ident = keep.tile([P, P], F32, name="ident")
         make_identity(nc, ident[:])
 
-
+        w_code, w_scale = [], []
         y_sb, a_sb, cap, ratio, plain = {}, {}, {}, {}, {}
+        blocks = [slice(b * P, (b + 1) * P) for b in range(S // P)]
+
+        def gather_adv(t):
+            a_sb[t] = keep.tile([P, S], F32, name=f"a{t}")
+            nc.vector.tensor_copy(a_sb[t][:], adv_table[t][:].indirect(st_sb[:]))
+
+        def quantize_weights(pair, cast):
+            grouped = keep.tile([P, PAIR, P, PACK], BF16, name=f"grouped{pair}", align_bytes=64)
+            columns = w_raw[:].rearrange("p j (c t) -> p c t j", t=TILES)[:, :, pair * PAIR : (pair + 1) * PAIR, :]
+            cast(grouped[:].rearrange("p i c j -> p c i j"), columns)
+            codes = keep.tile([P, PAIR * P], U32, name=f"w_code{pair}", align_bytes=64)
+            scales = keep.tile([P, PAIR * P], U8, name=f"w_scale{pair}", align_bytes=64)
+            nc.vector.quantize_mx(codes[:].bitcast(FP8X4), scales[:], grouped[:].rearrange("p i c j -> p (i c j)"))
+            w_code.append(codes)
+            w_scale.append(scales)
 
         def project(t):
+            pair, i = divmod(t, PAIR)
             y_ps = psum_y.tile([P, S], F32, name="y_ps")
-            h, i = divmod(t, TILES // HALVES)
-            cols = slice(i * P, (i + 1) * P)
             nc.tensor.matmul_mx(
                 y_ps[:],
-                lhsT=w_code[h][:, cols].bitcast(FP8X4),
-                lhsT_scale=w_scale[h][:, cols],
+                lhsT=w_code[pair][:, blocks[i]].bitcast(FP8X4),
+                lhsT_scale=w_scale[pair][:, blocks[i]],
                 rhs=x_code[:].bitcast(FP8X4),
                 rhs_scale=x_scale[:],
                 start=True,
                 stop=True,
             )
-            y_sb[t] = work.tile([P, S], F32, name="y_sb")
+            y_sb[t] = y_pool.tile([P, S], F32, name="y_sb")
             nc.scalar.copy(y_sb[t][:], y_ps[:])
 
-        def fetch_adv(t):
-            a_sb[t] = keep.tile([P, S], F32, name=f"a{t}")
-            nc.vector.tensor_copy(a_sb[t][:], adv_sb[t][:].indirect(st_sb[:]))
-
-        def bound(t):
-            turned = psum_t.tile([P, S], F32, name="turned")
-            for b in range(S // P):
-                blk = slice(b * P, (b + 1) * P)
-                nc.tensor.transpose(turned[:, blk], a_sb[t][:, blk], ident[:])
-            parts = keep.tile([P, 2 * S], F32, name=f"parts{t}", tag="w_raw0")
-            base, extra = parts[:, :S], parts[:, S:]
+        def make_cap(t, reuses):
+            turned = psum_turned.tile([P, S], F32, name="turned")
+            for block in blocks:
+                nc.tensor.transpose(turned[:, block], a_sb[t][:, block], ident[:])
+            terms = keep.tile([P, 2 * S], F32, name=f"terms{t}", tag=reuses)
+            base, extra = terms[:, :S], terms[:, S:]
             nc.scalar.activation(base, turned[:], ACT.Copy, scale=LOW)
             nc.scalar.activation(extra, turned[:], ACT.Relu, scale=HIGH - LOW)
-            cap[t] = psum_c.tile([P, S], F32, name="cap")
-            for b in range(S // P):
-                blk = slice(b * P, (b + 1) * P)
-                nc.tensor.matmul(cap[t][:, blk], base[:, blk], ident[:], start=True, stop=False, is_transpose=True)
-                nc.tensor.matmul(cap[t][:, blk], extra[:, blk], ident[:], start=False, stop=True, is_transpose=True)
+            cap[t] = psum_cap.tile([P, S], F32, name="cap")
+            for block in blocks:
+                nc.tensor.matmul(cap[t][:, block], base[:, block], ident[:], start=True, stop=False, is_transpose=True)
+                nc.tensor.matmul(cap[t][:, block], extra[:, block], ident[:], start=False, stop=True, is_transpose=True)
 
-        def fetch_old(t):
+        def make_ratio(t):
             diff = keep.tile([P, S], F32, name=f"diff{t}", tag=f"diff{t}")
-            nc.vector.tensor_tensor(diff[:], old_sb[t][:].indirect(st_sb[:]), y_sb[t][:], ALU.subtract)
+            nc.vector.tensor_tensor(diff[:], old_table[t][:].indirect(st_sb[:]), y_sb[t][:], ALU.subtract)
             ratio[t] = keep.tile([P, S], F32, name=f"ratio{t}")
             nc.scalar.activation(ratio[t][:], diff[:], ACT.Exp, scale=-0.25)
 
@@ -131,50 +129,33 @@ def tile_picked_ppo8_none_p_kernel(tc, x_words, x_scales, w1, old, adv, offs, st
             nc.vector.tensor_tensor(result[:], plain[t][:], cap[t][:], ALU.min)
             nc.sync.dma_start(out_rows[:, t, :], result[:])
 
-        fetch_adv(0)
-        fetch_adv(1)
+        gather_adv(0)
         x_scale = keep.tile([P, S], U8, name="x_scale", align_bytes=64)
         nc.vector.tensor_copy(x_scale[:], scale_table[:].indirect(offs_sb[:]))
-
-        w_code, w_scale = [], []
-        per_half = TILES // HALVES
-        w_cols = w_raw[:].rearrange("p j (m t) -> p m t j", t=TILES)
-        for h in range(HALVES):
-            grouped = keep.tile([P, per_half, P, PACK], BF16, name=f"grouped{h}", align_bytes=64)
-            dst = grouped[:].rearrange("p t m j -> p m t j")
-            src = w_cols[:, :, h * per_half : (h + 1) * per_half, :]
-            if h == 0:
-                nc.vector.tensor_copy(dst, src)
-            else:
-                nc.scalar.copy(dst, src)
-            codes = keep.tile([P, per_half * P], U32, name=f"w_code{h}", align_bytes=64)
-            scales = keep.tile([P, per_half * P], U8, name=f"w_scale{h}", align_bytes=64)
-            nc.vector.quantize_mx(codes[:].bitcast(FP8X4), scales[:], grouped[:].rearrange("p t m j -> p (t m j)"))
-            w_code.append(codes)
-            w_scale.append(scales)
-
+        quantize_weights(0, nc.vector.tensor_copy)
+        quantize_weights(1, nc.scalar.copy)
         x_code = keep.tile([P, S], U32, name="x_code", align_bytes=64)
         nc.vector.tensor_copy(x_code[:], word_table[:].bitcast(U32).indirect(offs_sb[:]))
-        bound(0)
-        bound(1)
+        make_cap(0, reuses="w_raw")
 
-        project(0)
-        project(1)
-        fetch_adv(2)
-        fetch_adv(3)
-        bound(2)
-        fetch_old(0)
-        project(2)
-        fetch_old(1)
-        bound(3)
-        project(3)
-        multiply(0)
-        fetch_old(2)
-        finish(0)
-        multiply(1)
-        fetch_old(3)
-        finish(1)
-        multiply(2)
-        multiply(3)
-        finish(2)
-        finish(3)
+        for t in range(Y_BUFFERS):
+            project(t)
+        for t in range(1, TILES):
+            gather_adv(t)
+        make_cap(1, reuses="terms1")
+
+        make_ratio(0)
+        for t in range(Y_BUFFERS, TILES):
+            project(t)
+        make_ratio(1)
+        for t in range(2, TILES):
+            make_cap(t, reuses=f"diff{t - 2}")
+
+        for t in range(TILES - 2):
+            multiply(t)
+            make_ratio(t + 2)
+            finish(t)
+        for t in range(TILES - 2, TILES):
+            multiply(t)
+        for t in range(TILES - 2, TILES):
+            finish(t)

@@ -22,54 +22,54 @@ QUADRANTS = 4
 TILES = N // P
 PAIR = 2
 LOW, HIGH = 0.8, 1.25
-Y_BUFFERS = 3
+Y_BUFFERS = 4
 
 
 def tile_picked_ppo8_none_p_kernel(tc, x_words, x_scales, w1, old, adv, offs, st, out):
     nc = tc.nc
     with ExitStack() as ctx:
         keep = ctx.enter_context(tc.tile_pool(name="keep", bufs=1))
-        y_pool = ctx.enter_context(tc.tile_pool(name="y_pool", bufs=Y_BUFFERS))
-        psum_y = ctx.enter_context(tc.psum_pool(name="psum_y", bufs=2))
-        psum_turned = ctx.enter_context(tc.psum_pool(name="psum_turned", bufs=2))
-        psum_cap = ctx.enter_context(tc.psum_pool(name="psum_cap", bufs=TILES))
+        psum = ctx.enter_context(tc.psum_pool(name="psum", bufs=1))
 
         offs_sb = keep.tile([P, S // 16], U16, name="offs_sb")
         st_sb = keep.tile([P, S // 16], U16, name="st_sb")
-        nc.sync.dma_start(offs_sb[:], offs)
-        nc.sync.dma_start(st_sb[:], st)
-
-        scale_table = keep.tile([P, T], U8, name="scale_table")
-        nc.gpsimd.memset(scale_table[:].bitcast(I32), 0)
-        scale_rows = keep.tile([P, T // 4], I32, name="scale_rows")
-        for q in range(QUADRANTS):
-            nc.sync.dma_start(scale_rows[32 * q : 32 * q + 4, :], x_scales[0, 4 * q : 4 * q + 4, :].bitcast(I32))
-        for q in range(QUADRANTS):
-            live = slice(32 * q, 32 * q + 4)
-            nc.vector.tensor_copy(scale_table[live, :].bitcast(I32), scale_rows[live, :])
+        scale_table = keep.tile([P, T // 4], I32, name="scale_table")
+        nc.gpsimd.memset(scale_table[:], 0)
 
         old_rows = old.rearrange("(p t) u -> p t u", t=TILES)
         adv_rows = adv.rearrange("(p t) u -> p t u", t=TILES)
         out_rows = out.rearrange("(p t) s -> p t s", t=TILES)
 
         def load_table(rows, t, name):
-            table = keep.tile([P, U], F32, name=name)
+            table = keep.tile([P, U], F32, name=name, tag=name)
             nc.sync.dma_start(table[:], rows[:, t, :])
             return table
 
-        adv_table = [load_table(adv_rows, 0, "adv0")]
+        scale_rows = keep.tile([P, T // 4], I32, name="scale_rows")
+        for r in range(4):
+            nc.sync.dma_start(scale_rows[r:P:32, :], x_scales[0, r:16:4, :].bitcast(I32))
+        for q in range(QUADRANTS):
+            live = slice(32 * q, 32 * q + 4)
+            nc.vector.tensor_copy(scale_table[live, :], scale_rows[live, :])
+        nc.sync.dma_start(st_sb[:], st)
+        nc.sync.dma_start(offs_sb[:], offs)
+        adv_table, old_table = {0: load_table(adv_rows, 0, "adv0")}, {}
         w_raw = keep.tile([P, PACK, N], F32, name="w_raw", tag="w_raw")
         nc.sync.dma_start(w_raw[:], w1.rearrange("(p j) m -> p j m", j=PACK))
         word_table = keep.tile([P, T], I32, name="word_table")
         nc.sync.dma_start(word_table[:], x_words[0].rearrange("p n r -> p (n r)").bitcast(I32))
-        adv_table.extend(load_table(adv_rows, t, f"adv{t}") for t in range(1, TILES))
-        old_table = [load_table(old_rows, t, f"old{t}") for t in range(TILES)]
+        for kind, t in (("a", 1), ("o", 0), ("o", 1), ("a", 2), ("a", 3), ("o", 2), ("o", 3)):
+            if kind == "a":
+                adv_table[t] = load_table(adv_rows, t, f"adv{t}")
+            else:
+                old_table[t] = load_table(old_rows, t, f"old{t}")
 
         ident = keep.tile([P, P], F32, name="ident")
         make_identity(nc, ident[:])
 
         w_code, w_scale = [], []
-        y_sb, a_sb, cap, ratio, plain = {}, {}, {}, {}, {}
+        a_sb, cap, plain = {}, {}, {}
+        turned, base, extra = {}, {}, {}
         blocks = [slice(b * P, (b + 1) * P) for b in range(S // P)]
 
         def gather_adv(t):
@@ -86,76 +86,112 @@ def tile_picked_ppo8_none_p_kernel(tc, x_words, x_scales, w1, old, adv, offs, st
             w_code.append(codes)
             w_scale.append(scales)
 
-        def project(t):
+        def project(t, parts, bank):
             pair, i = divmod(t, PAIR)
-            y_ps = psum_y.tile([P, S], F32, name="y_ps")
-            nc.tensor.matmul_mx(
-                y_ps[:],
-                lhsT=w_code[pair][:, blocks[i]].bitcast(FP8X4),
-                lhsT_scale=w_scale[pair][:, blocks[i]],
-                rhs=x_code[:].bitcast(FP8X4),
-                rhs_scale=x_scale[:],
-                start=True,
-                stop=True,
-            )
-            y_sb[t] = y_pool.tile([P, S], F32, name="y_sb")
-            nc.scalar.copy(y_sb[t][:], y_ps[:])
+            y_ps = psum.tile([P, S], F32, name="y_ps", tag=f"bank{bank}")
+            for part in parts:
+                nc.tensor.matmul_mx(
+                    y_ps[:, part],
+                    lhsT=w_code[pair][:, blocks[i]].bitcast(FP8X4),
+                    lhsT_scale=w_scale[pair][:, blocks[i]],
+                    rhs=x_code[:, part].bitcast(FP8X4),
+                    rhs_scale=x_scale[:, part],
+                    start=True,
+                    stop=True,
+                )
+            return y_ps
 
-        def make_cap(t, reuses):
-            turned = psum_turned.tile([P, S], F32, name="turned")
+        def copy_y(y_ps, part, name):
+            y = keep.tile([P, part.stop - part.start], F32, name=name, tag=name)
+            nc.scalar.copy(y[:], y_ps[:, part])
+            return y
+
+        def turn(t):
+            turned[t] = psum.tile([P, S], F32, name="turned", tag=f"bank{4 + t % 2}")
             for block in blocks:
-                nc.tensor.transpose(turned[:, block], a_sb[t][:, block], ident[:])
-            terms = keep.tile([P, 2 * S], F32, name=f"terms{t}", tag=reuses)
-            base, extra = terms[:, :S], terms[:, S:]
-            nc.scalar.activation(base, turned[:], ACT.Copy, scale=LOW)
-            nc.scalar.activation(extra, turned[:], ACT.Relu, scale=HIGH - LOW)
-            cap[t] = psum_cap.tile([P, S], F32, name="cap")
+                nc.tensor.transpose(turned[t][:, block], a_sb[t][:, block], ident[:])
+
+        def make_terms(t):
+            base[t] = keep.tile([P, S], F32, name=f"base{t}", tag="w_raw" if t == 0 else f"base{t}")
+            extra[t] = keep.tile([P, S], F32, name=f"extra{t}")
+            nc.scalar.activation(base[t][:], turned[t][:], ACT.Copy, scale=LOW)
+            nc.scalar.activation(extra[t][:], turned[t][:], ACT.Relu, scale=HIGH - LOW)
+
+        def make_cap(t):
+            cap[t] = psum.tile([P, S], F32, name="cap", tag=f"bank{(1, 6, 7, 2)[t]}")
             for block in blocks:
-                nc.tensor.matmul(cap[t][:, block], base[:, block], ident[:], start=True, stop=False, is_transpose=True)
-                nc.tensor.matmul(cap[t][:, block], extra[:, block], ident[:], start=False, stop=True, is_transpose=True)
+                nc.tensor.matmul(cap[t][:, block], extra[t][:, block], ident[:], start=True, stop=False, is_transpose=True)
+                nc.tensor.matmul(cap[t][:, block], base[t][:, block], ident[:], start=False, stop=True, is_transpose=True)
 
-        def make_ratio(t):
-            diff = keep.tile([P, S], F32, name=f"diff{t}", tag=f"diff{t}")
-            nc.vector.tensor_tensor(diff[:], old_table[t][:].indirect(st_sb[:]), y_sb[t][:], ALU.subtract)
-            ratio[t] = keep.tile([P, S], F32, name=f"ratio{t}")
-            nc.scalar.activation(ratio[t][:], diff[:], ACT.Exp, scale=-0.25)
+        def make_ratio(t, part, y):
+            entries = st_sb[:, part.start // 16 : part.stop // 16]
+            nc.vector.tensor_tensor(diff[t][:, part], old_table[t][:].indirect(entries), y, ALU.subtract)
+            nc.scalar.activation(ratio[t][:, part], diff[t][:, part], ACT.Exp, scale=-0.25)
 
-        def multiply(t):
-            plain[t] = keep.tile([P, S], F32, name=f"plain{t}")
-            nc.vector.tensor_tensor(plain[t][:], ratio[t][:], a_sb[t][:], ALU.mult)
+        def multiply(t, engine, part):
+            engine.tensor_tensor(plain[t][:, part], ratio[t][:, part], a_sb[t][:, part], ALU.mult)
 
-        def finish(t):
-            result = keep.tile([P, S], F32, name=f"result{t}")
-            nc.vector.tensor_tensor(result[:], plain[t][:], cap[t][:], ALU.min)
-            nc.sync.dma_start(out_rows[:, t, :], result[:])
+        def finish(t, part):
+            nc.vector.tensor_tensor(result[t][:, part], plain[t][:, part], cap[t][:, part], ALU.min)
+            nc.sync.dma_start(out_rows[:, t, part], result[t][:, part])
+
+        whole = slice(0, S)
+        halves = [slice(0, S // 2), slice(S // 2, S)]
+        diff = [keep.tile([P, S], F32, name=f"diff{t}") for t in range(TILES)]
+        ratio = [keep.tile([P, S], F32, name=f"ratio{t}") for t in range(TILES)]
 
         gather_adv(0)
         x_scale = keep.tile([P, S], U8, name="x_scale", align_bytes=64)
-        nc.vector.tensor_copy(x_scale[:], scale_table[:].indirect(offs_sb[:]))
+        nc.vector.tensor_copy(x_scale[:], scale_table[:].bitcast(U8).indirect(offs_sb[:]))
         quantize_weights(0, nc.vector.tensor_copy)
         quantize_weights(1, nc.scalar.copy)
         x_code = keep.tile([P, S], U32, name="x_code", align_bytes=64)
-        nc.vector.tensor_copy(x_code[:], word_table[:].bitcast(U32).indirect(offs_sb[:]))
-        make_cap(0, reuses="w_raw")
-
-        for t in range(Y_BUFFERS):
-            project(t)
-        for t in range(1, TILES):
-            gather_adv(t)
-        make_cap(1, reuses="terms1")
-
-        make_ratio(0)
-        for t in range(Y_BUFFERS, TILES):
-            project(t)
-        make_ratio(1)
-        for t in range(2, TILES):
-            make_cap(t, reuses=f"diff{t - 2}")
-
-        for t in range(TILES - 2):
-            multiply(t)
-            make_ratio(t + 2)
-            finish(t)
-        for t in range(TILES - 2, TILES):
-            multiply(t)
-        for t in range(TILES - 2, TILES):
-            finish(t)
+        for part in halves:
+            entries = offs_sb[:, part.start // 16 : part.stop // 16]
+            nc.vector.tensor_copy(x_code[:, part], word_table[:].bitcast(U32).indirect(entries))
+        turn(0)
+        y0 = keep.tile([P, S], F32, name="y0")
+        y0_ps = [project(0, [part], h) for h, part in enumerate(halves)]
+        for part, y_ps in zip(halves, y0_ps):
+            nc.scalar.copy(y0[:, part], y_ps[:, part])
+        y1 = copy_y(project(1, [whole], 2), whole, "y1")
+        y2 = copy_y(project(2, [whole], 3), whole, "y2")
+        y3_ps = project(3, [whole], 0)
+        y3 = [copy_y(y3_ps, part, f"y3_{h}") for h, part in enumerate(halves)]
+        gather_adv(1)
+        make_terms(0)
+        turn(1)
+        make_cap(0)
+        make_ratio(0, whole, y0[:])
+        make_ratio(1, whole, y1[:])
+        plain[0] = keep.tile([P, S], F32, name="plain0", tag="y1")
+        plain[1] = keep.tile([P, S], F32, name="plain1")
+        multiply(0, nc.gpsimd, whole)
+        multiply(1, nc.gpsimd, whole)
+        make_terms(1)
+        gather_adv(2)
+        gather_adv(3)
+        turn(2)
+        turn(3)
+        result = {0: keep.tile([P, S], F32, name="result0", tag="adv3")}
+        finish(0, whole)
+        make_ratio(2, whole, y2[:])
+        for part, y in zip(halves, y3):
+            make_ratio(3, part, y[:])
+        late = keep.tile([P, 2, S], F32, name="late", tag="y3_0")
+        result[1], plain[2] = late[:, 0, :], late[:, 1, :]
+        plain[3] = keep.tile([P, S], F32, name="plain3")
+        for t in (2, 3):
+            result[t] = keep.tile([P, S], F32, name=f"result{t}")
+        make_cap(1)
+        make_terms(2)
+        make_terms(3)
+        make_cap(2)
+        make_cap(3)
+        finish(1, whole)
+        multiply(2, nc.vector, whole)
+        multiply(3, nc.vector, halves[0])
+        finish(2, whole)
+        multiply(3, nc.vector, halves[1])
+        finish(3, halves[0])
+        finish(3, halves[1])

@@ -52,8 +52,8 @@ def tile_picked_ppo8_none_p_kernel(tc, x_words, x_scales, w1, old, adv, offs, st
             live = slice(32 * q, 32 * q + 4)
             nc.vector.tensor_copy(scale_table[live, :], scale_rows[live, :])
         nc.sync.dma_start(st_sb[:], st)
-        nc.sync.dma_start(offs_sb[:], offs)
         adv_table, old_table = {0: load_table(adv_rows, 0, "adv0")}, {}
+        nc.sync.dma_start(offs_sb[:], offs)
         w_raw = keep.tile([P, PACK, N], F32, name="w_raw", tag="w_raw")
         nc.sync.dma_start(w_raw[:], w1.rearrange("(p j) m -> p j m", j=PACK))
         word_table = keep.tile([P, T], I32, name="word_table")
@@ -76,10 +76,11 @@ def tile_picked_ppo8_none_p_kernel(tc, x_words, x_scales, w1, old, adv, offs, st
             a_sb[t] = keep.tile([P, S], F32, name=f"a{t}")
             nc.vector.tensor_copy(a_sb[t][:], adv_table[t][:].indirect(st_sb[:]))
 
-        def quantize_weights(pair, cast):
+        def quantize_weights(pair, casts):
             grouped = keep.tile([P, PAIR, P, PACK], BF16, name=f"grouped{pair}", align_bytes=64)
             columns = w_raw[:].rearrange("p j (c t) -> p c t j", t=TILES)[:, :, pair * PAIR : (pair + 1) * PAIR, :]
-            cast(grouped[:].rearrange("p i c j -> p c i j"), columns)
+            for cast, tiles in casts:
+                cast(grouped[:, tiles].rearrange("p i c j -> p c i j"), columns[:, :, tiles, :])
             codes = keep.tile([P, PAIR * P], U32, name=f"w_code{pair}", align_bytes=64)
             scales = keep.tile([P, PAIR * P], U8, name=f"w_scale{pair}", align_bytes=64)
             nc.vector.quantize_mx(codes[:].bitcast(FP8X4), scales[:], grouped[:].rearrange("p i c j -> p (i c j)"))
@@ -112,86 +113,105 @@ def tile_picked_ppo8_none_p_kernel(tc, x_words, x_scales, w1, old, adv, offs, st
                 nc.tensor.transpose(turned[t][:, block], a_sb[t][:, block], ident[:])
 
         def make_terms(t):
-            base[t] = keep.tile([P, S], F32, name=f"base{t}", tag="w_raw" if t == 0 else f"base{t}")
-            extra[t] = keep.tile([P, S], F32, name=f"extra{t}")
-            nc.scalar.activation(base[t][:], turned[t][:], ACT.Copy, scale=LOW)
-            nc.scalar.activation(extra[t][:], turned[t][:], ACT.Relu, scale=HIGH - LOW)
+            nc.scalar.activation(base[t][:, :], turned[t][:], ACT.Copy, scale=LOW)
+            nc.scalar.activation(extra[t][:, :], turned[t][:], ACT.Relu, scale=HIGH - LOW)
 
         def make_cap(t):
-            cap[t] = psum.tile([P, S], F32, name="cap", tag=f"bank{(1, 6, 7, 2)[t]}")
-            for block in blocks:
-                nc.tensor.matmul(cap[t][:, block], extra[t][:, block], ident[:], start=True, stop=False, is_transpose=True)
-                nc.tensor.matmul(cap[t][:, block], base[t][:, block], ident[:], start=False, stop=True, is_transpose=True)
+            cap[t] = psum.tile([P, S], F32, name="cap", tag=f"bank{(6, 7, 1, 2)[t]}")
+            passes = [(term, block) for term in (base[t], extra[t]) for block in blocks]
+            for n, (term, block) in enumerate(passes):
+                first, last = n == 0, n == len(passes) - 1
+                nc.tensor.matmul(cap[t][:, block], term[:, block], ident[:], start=first, stop=last, is_transpose=True)
 
         def make_ratio(t, part, y):
             entries = st_sb[:, part.start // 16 : part.stop // 16]
             nc.vector.tensor_tensor(diff[t][:, part], old_table[t][:].indirect(entries), y, ALU.subtract)
             nc.scalar.activation(ratio[t][:, part], diff[t][:, part], ACT.Exp, scale=-0.25)
 
-        def multiply(t, engine, part):
-            engine.tensor_tensor(plain[t][:, part], ratio[t][:, part], a_sb[t][:, part], ALU.mult)
+        def multiply(t):
+            nc.gpsimd.tensor_tensor(plain[t][:], ratio[t][:], a_sb[t][:], ALU.mult)
 
-        def finish(t, part):
-            nc.vector.tensor_tensor(result[t][:, part], plain[t][:, part], cap[t][:, part], ALU.min)
+        def multiply_last(part, product):
+            nc.vector.scalar_tensor_tensor(product, ratio[3][:, part], 1.0 / LOW, base_ps[:, part], ALU.mult, ALU.mult)
+
+        def finish(t, part, product):
+            nc.vector.tensor_tensor(result[t][:, part], product, cap[t][:, part], ALU.min)
             nc.sync.dma_start(out_rows[:, t, part], result[t][:, part])
 
         whole = slice(0, S)
         halves = [slice(0, S // 2), slice(S // 2, S)]
-        diff = [keep.tile([P, S], F32, name=f"diff{t}") for t in range(TILES)]
+        diff = [keep.tile([P, S], F32, name=f"diff{t}", tag=f"diff{t}") for t in range(TILES)]
         ratio = [keep.tile([P, S], F32, name=f"ratio{t}") for t in range(TILES)]
 
         gather_adv(0)
+        turn(0)
         x_scale = keep.tile([P, S], U8, name="x_scale", align_bytes=64)
         nc.vector.tensor_copy(x_scale[:], scale_table[:].bitcast(U8).indirect(offs_sb[:]))
-        quantize_weights(0, nc.vector.tensor_copy)
-        quantize_weights(1, nc.scalar.copy)
+        quantize_weights(0, [(nc.vector.tensor_copy, slice(0, 2))])
+        quantize_weights(1, [(nc.scalar.copy, slice(0, 2))])
+        base[0] = keep.tile([P, S], F32, name="base0")
+        extra[0] = keep.tile([P, S], F32, name="extra0", tag="w_raw")
+        make_terms(0)
+        make_cap(0)
         x_code = keep.tile([P, S], U32, name="x_code", align_bytes=64)
         for part in halves:
             entries = offs_sb[:, part.start // 16 : part.stop // 16]
             nc.vector.tensor_copy(x_code[:, part], word_table[:].bitcast(U32).indirect(entries))
-        turn(0)
-        y0 = keep.tile([P, S], F32, name="y0")
+        y0 = keep.tile([P, S], F32, name="y0", tag="y0")
         y0_ps = [project(0, [part], h) for h, part in enumerate(halves)]
         for part, y_ps in zip(halves, y0_ps):
             nc.scalar.copy(y0[:, part], y_ps[:, part])
         y1 = copy_y(project(1, [whole], 2), whole, "y1")
-        y2 = copy_y(project(2, [whole], 3), whole, "y2")
+        y2_ps = project(2, [whole], 3)
         y3_ps = project(3, [whole], 0)
-        y3 = [copy_y(y3_ps, part, f"y3_{h}") for h, part in enumerate(halves)]
         gather_adv(1)
-        make_terms(0)
         turn(1)
-        make_cap(0)
         make_ratio(0, whole, y0[:])
         make_ratio(1, whole, y1[:])
+        base[1] = keep.tile([P, S], F32, name="base1")
+        extra[1] = keep.tile([P, S], F32, name="extra1")
+        make_terms(1)
+        y_late = keep.tile([P, S + S // 2], F32, name="y_late", tag="diff0")
+        y3_first = keep.tile([P, S // 2], F32, name="y3_first", tag="diff1")
+        y2, y3 = y_late[:, :S], [y3_first[:, :], y_late[:, S:]]
+        nc.scalar.copy(y2, y2_ps[:])
+        for part, y in zip(halves, y3):
+            nc.scalar.copy(y, y3_ps[:, part])
         plain[0] = keep.tile([P, S], F32, name="plain0", tag="y1")
         plain[1] = keep.tile([P, S], F32, name="plain1")
-        multiply(0, nc.gpsimd, whole)
-        multiply(1, nc.gpsimd, whole)
-        make_terms(1)
+        multiply(0)
+        multiply(1)
+        make_cap(1)
         gather_adv(2)
         gather_adv(3)
         turn(2)
         turn(3)
-        result = {0: keep.tile([P, S], F32, name="result0", tag="adv3")}
-        finish(0, whole)
-        make_ratio(2, whole, y2[:])
-        for part, y in zip(halves, y3):
-            make_ratio(3, part, y[:])
-        late = keep.tile([P, 2, S], F32, name="late", tag="y3_0")
-        result[1], plain[2] = late[:, 0, :], late[:, 1, :]
-        plain[3] = keep.tile([P, S], F32, name="plain3")
-        for t in (2, 3):
-            result[t] = keep.tile([P, S], F32, name=f"result{t}")
-        make_cap(1)
+        behind_adv = keep.tile([P, 3, S], F32, name="behind_adv", tag="adv3")
+        base[2], extra[2] = behind_adv[:, 0, :], behind_adv[:, 1, :]
+        result = {0: behind_adv[:, 2, :]}
+        finish(0, whole, plain[0][:])
+        base[3] = keep.tile([P, S], F32, name="base3")
+        extra[3] = keep.tile([P, S], F32, name="extra3")
         make_terms(2)
         make_terms(3)
+        make_ratio(2, whole, y2)
+        for part, y in zip(halves, y3):
+            make_ratio(3, part, y)
+        result[1] = keep.tile([P, S], F32, name="result1", tag="diff1")
+        plain[2] = keep.tile([P, S], F32, name="plain2", tag="diff0")
+        last = [keep.tile([P, S // 2], F32, name=f"plain3_{h}", tag=f"plain3_{h}") for h in range(2)]
+        result[3] = keep.tile([P, S], F32, name="result3")
+        multiply(2)
         make_cap(2)
+        base_ps = psum.tile([P, S], F32, name="base_ps", tag="bank3")
+        for block in blocks:
+            nc.tensor.transpose(base_ps[:, block], base[3][:, block], ident[:])
         make_cap(3)
-        finish(1, whole)
-        multiply(2, nc.vector, whole)
-        multiply(3, nc.vector, halves[0])
-        finish(2, whole)
-        multiply(3, nc.vector, halves[1])
-        finish(3, halves[0])
-        finish(3, halves[1])
+        finish(1, whole, plain[1][:])
+        for part, product in zip(halves, last):
+            multiply_last(part, product[:])
+        for part, product in zip(halves, last):
+            finish(3, part, product[:])
+        result[2] = keep.tile([P, S], F32, name="result2", tag="plain3_0")
+        for part in halves:
+            finish(2, part, plain[2][:, part])

@@ -33,36 +33,39 @@ def tile_picked_ppo8_none_p_kernel(tc, x_words, x_scales, w1, old, adv, offs, st
 
         offs_sb = keep.tile([P, S // 16], U16, name="offs_sb")
         st_sb = keep.tile([P, S // 16], U16, name="st_sb")
-        scale_table = keep.tile([P, T // 4], I32, name="scale_table")
+        shared = ctx.enter_context(tc.tile_pool(name="shared", bufs=1))
+        TABLE = 4 * U
+        place = {"scale_table": 0, "adv1": 0, "old3": 0, "adv0": TABLE, "old0": TABLE, "w_raw": 2 * TABLE, "old1": 2 * TABLE,
+                 "adv2": 3 * TABLE, "word_table": 4 * TABLE, "old2": 4 * TABLE, "adv3": 5 * TABLE, "behind_adv": 5 * TABLE}
+
+        scale_table = shared.tile([P, T // 4], I32, name="scale_table", offset=place["scale_table"])
         nc.gpsimd.memset(scale_table[:], 0)
+        x_scale = keep.tile([P, S // 4], I32, name="x_scale", align_bytes=64)
+        nc.gpsimd.memset(x_scale[:], 0)
 
         old_rows = old.rearrange("(p t) u -> p t u", t=TILES)
         adv_rows = adv.rearrange("(p t) u -> p t u", t=TILES)
         out_rows = out.rearrange("(p t) s -> p t s", t=TILES)
 
         def load_table(rows, t, name):
-            table = keep.tile([P, U], F32, name=name, tag=name)
+            table = shared.tile([P, U], F32, name=name, offset=place[name])
             nc.sync.dma_start(table[:], rows[:, t, :])
             return table
 
-        scale_rows = keep.tile([P, T // 4], I32, name="scale_rows")
-        for r in range(4):
-            nc.sync.dma_start(scale_rows[r:P:32, :], x_scales[0, r:16:4, :].bitcast(I32))
-        for q in range(QUADRANTS):
-            live = slice(32 * q, 32 * q + 4)
-            nc.vector.tensor_copy(scale_table[live, :], scale_rows[live, :])
-        nc.sync.dma_start(st_sb[:], st)
-        adv_table, old_table = {0: load_table(adv_rows, 0, "adv0")}, {}
+        scale_rows = keep.tile([16, T // 4], I32, name="scale_rows")
+        nc.sync.dma_start(scale_rows[:], x_scales[0].bitcast(I32))
+        nc.vector.tensor_copy(scale_table[:16, :], scale_rows[:])
         nc.sync.dma_start(offs_sb[:], offs)
-        w_raw = keep.tile([P, PACK, N], F32, name="w_raw", tag="w_raw")
+        adv_table, old_table = {0: load_table(adv_rows, 0, "adv0")}, {}
+        nc.sync.dma_start(st_sb[:], st)
+        w_raw = shared.tile([P, PACK, N], F32, name="w_raw", offset=place["w_raw"])
         nc.sync.dma_start(w_raw[:], w1.rearrange("(p j) m -> p j m", j=PACK))
-        word_table = keep.tile([P, T], I32, name="word_table")
+        word_table = shared.tile([P, T], I32, name="word_table", offset=place["word_table"])
         nc.sync.dma_start(word_table[:], x_words[0].rearrange("p n r -> p (n r)").bitcast(I32))
-        for kind, t in (("a", 1), ("o", 0), ("o", 1), ("a", 2), ("a", 3), ("o", 2), ("o", 3)):
-            if kind == "a":
-                adv_table[t] = load_table(adv_rows, t, f"adv{t}")
-            else:
-                old_table[t] = load_table(old_rows, t, f"old{t}")
+        picked_scales = keep.tile([P, S], U8, name="picked_scales")
+        nc.vector.tensor_copy(picked_scales[:], scale_table[:].bitcast(U8).indirect(offs_sb[:]))
+        for q in range(QUADRANTS):
+            nc.sync.dma_start(x_scale[32 * q : 32 * q + 4, :], picked_scales[4 * q : 4 * q + 4, :].bitcast(I32))
 
         ident = keep.tile([P, P], F32, name="ident")
         make_identity(nc, ident[:])
@@ -96,7 +99,7 @@ def tile_picked_ppo8_none_p_kernel(tc, x_words, x_scales, w1, old, adv, offs, st
                     lhsT=w_code[pair][:, blocks[i]].bitcast(FP8X4),
                     lhsT_scale=w_scale[pair][:, blocks[i]],
                     rhs=x_code[:, part].bitcast(FP8X4),
-                    rhs_scale=x_scale[:, part],
+                    rhs_scale=x_scale[:].bitcast(U8)[:, part],
                     start=True,
                     stop=True,
                 )
@@ -145,18 +148,22 @@ def tile_picked_ppo8_none_p_kernel(tc, x_words, x_scales, w1, old, adv, offs, st
 
         gather_adv(0)
         turn(0)
-        x_scale = keep.tile([P, S], U8, name="x_scale", align_bytes=64)
-        nc.vector.tensor_copy(x_scale[:], scale_table[:].bitcast(U8).indirect(offs_sb[:]))
+        adv_table[1] = load_table(adv_rows, 1, "adv1")
+        old_table[0] = load_table(old_rows, 0, "old0")
         quantize_weights(0, [(nc.vector.tensor_copy, slice(0, 2))])
         quantize_weights(1, [(nc.scalar.copy, slice(0, 2))])
+        old_table[1] = load_table(old_rows, 1, "old1")
+        adv_table[2] = load_table(adv_rows, 2, "adv2")
         base[0] = keep.tile([P, S], F32, name="base0")
-        extra[0] = keep.tile([P, S], F32, name="extra0", tag="w_raw")
+        extra[0] = keep.tile([P, S], F32, name="extra0")
         make_terms(0)
         make_cap(0)
         x_code = keep.tile([P, S], U32, name="x_code", align_bytes=64)
         for part in halves:
             entries = offs_sb[:, part.start // 16 : part.stop // 16]
             nc.vector.tensor_copy(x_code[:, part], word_table[:].bitcast(U32).indirect(entries))
+        adv_table[3] = load_table(adv_rows, 3, "adv3")
+        old_table[2] = load_table(old_rows, 2, "old2")
         y0 = keep.tile([P, S], F32, name="y0", tag="y0")
         y0_ps = [project(0, [part], h) for h, part in enumerate(halves)]
         for part, y_ps in zip(halves, y0_ps):
@@ -165,6 +172,7 @@ def tile_picked_ppo8_none_p_kernel(tc, x_words, x_scales, w1, old, adv, offs, st
         y2_ps = project(2, [whole], 3)
         y3_ps = project(3, [whole], 0)
         gather_adv(1)
+        old_table[3] = load_table(old_rows, 3, "old3")
         turn(1)
         make_ratio(0, whole, y0[:])
         make_ratio(1, whole, y1[:])
@@ -186,7 +194,7 @@ def tile_picked_ppo8_none_p_kernel(tc, x_words, x_scales, w1, old, adv, offs, st
         gather_adv(3)
         turn(2)
         turn(3)
-        behind_adv = keep.tile([P, 3, S], F32, name="behind_adv", tag="adv3")
+        behind_adv = shared.tile([P, 3, S], F32, name="behind_adv", offset=place["behind_adv"])
         base[2], extra[2] = behind_adv[:, 0, :], behind_adv[:, 1, :]
         result = {0: behind_adv[:, 2, :]}
         finish(0, whole, plain[0][:])

@@ -53,7 +53,7 @@ def tile_picked_ppo8_none_p_kernel(tc, x_words, x_scales, w1, old, adv, offs, st
             return table
 
         scale_rows = keep.tile([16, T // 4], I32, name="scale_rows")
-        nc.sync.dma_start(scale_rows[:], x_scales[0].bitcast(I32))
+        nc.scalar.dma_start(scale_rows[:], x_scales[0].bitcast(I32))
         nc.vector.tensor_copy(scale_table[:16, :], scale_rows[:])
         nc.sync.dma_start(offs_sb[:], offs)
         adv_table, old_table = {0: load_table(adv_rows, 0, "adv0")}, {}

@@ -169,20 +169,18 @@ def tile_picked_ppo8_none_p_kernel(tc, x_words, x_scales, w1, old, adv, offs, st
         for part, y_ps in zip(halves, y0_ps):
             nc.scalar.copy(y0[:, part], y_ps[:, part])
         y1 = copy_y(project(1, [whole], 2), whole, "y1")
-        y2_ps = project(2, [whole], 3)
+        y2 = copy_y(project(2, [whole], 3), whole, "y2")[:]
         y3_ps = project(3, [whole], 0)
         gather_adv(1)
         old_table[3] = load_table(old_rows, 3, "old3")
         turn(1)
         make_ratio(0, whole, y0[:])
         make_ratio(1, whole, y1[:])
-        base[1] = keep.tile([P, S], F32, name="base1")
-        extra[1] = keep.tile([P, S], F32, name="extra1")
+        y_late = keep.tile([P, 2 * S + S // 2], F32, name="y_late", tag="diff0")
+        base[1], extra[1] = y_late[:, :S], y_late[:, S + S // 2 :]
         make_terms(1)
-        y_late = keep.tile([P, S + S // 2], F32, name="y_late", tag="diff0")
         y3_first = keep.tile([P, S // 2], F32, name="y3_first", tag="diff1")
-        y2, y3 = y_late[:, :S], [y3_first[:, :], y_late[:, S:]]
-        nc.scalar.copy(y2, y2_ps[:])
+        y3 = [y3_first[:, :], y_late[:, S : S + S // 2]]
         for part, y in zip(halves, y3):
             nc.scalar.copy(y, y3_ps[:, part])
         plain[0] = keep.tile([P, S], F32, name="plain0", tag="y1")

@@ -1,7 +1,6 @@
 from contextlib import ExitStack
 
 import concourse.mybir as mybir
-from concourse.masks import make_identity
 
 K, T, S, N, U = 512, 2048, 512, 512, 1024
 FLOPS = 2 * K * N * S
@@ -22,7 +21,7 @@ QUADRANTS = 4
 TILES = N // P
 PAIR = 2
 LOW, HIGH = 0.8, 1.25
-Y_BUFFERS = 4
+TABLE = 4 * U
 
 
 def tile_picked_ppo8_none_p_kernel(tc, x_words, x_scales, w1, old, adv, offs, st, out):
@@ -30,13 +29,15 @@ def tile_picked_ppo8_none_p_kernel(tc, x_words, x_scales, w1, old, adv, offs, st
     with ExitStack() as ctx:
         keep = ctx.enter_context(tc.tile_pool(name="keep", bufs=1))
         psum = ctx.enter_context(tc.psum_pool(name="psum", bufs=1))
-
         offs_sb = keep.tile([P, S // 16], U16, name="offs_sb")
         st_sb = keep.tile([P, S // 16], U16, name="st_sb")
         shared = ctx.enter_context(tc.tile_pool(name="shared", bufs=1))
-        TABLE = 4 * U
-        place = {"scale_table": 0, "adv1": 0, "old3": 0, "adv0": TABLE, "old0": TABLE, "w_raw": 2 * TABLE, "old1": 2 * TABLE,
-                 "adv2": 3 * TABLE, "word_table": 4 * TABLE, "old2": 4 * TABLE, "adv3": 5 * TABLE, "behind_adv": 5 * TABLE}
+        place = {
+            "scale_table": 3 * TABLE // 4, "old0": 0, "adv0": TABLE, "ratio0": TABLE,
+            "w_raw": 2 * TABLE, "old1": 2 * TABLE, "adv1": 3 * TABLE, "ratio1": 3 * TABLE,
+            "word_table": 4 * TABLE, "old2": 4 * TABLE, "adv2": 5 * TABLE, "ratio2": 5 * TABLE,
+            "old3": 0, "adv3": 6 * TABLE, "ratio3": 6 * TABLE, "picked_old0": 6 * TABLE,
+        }
 
         scale_table = shared.tile([P, T // 4], I32, name="scale_table", offset=place["scale_table"])
         nc.gpsimd.memset(scale_table[:], 0)
@@ -56,10 +57,9 @@ def tile_picked_ppo8_none_p_kernel(tc, x_words, x_scales, w1, old, adv, offs, st
         nc.scalar.dma_start(scale_rows[:], x_scales[0].bitcast(I32))
         nc.vector.tensor_copy(scale_table[:16, :], scale_rows[:])
         nc.sync.dma_start(offs_sb[:], offs)
-        adv_table, old_table = {0: load_table(adv_rows, 0, "adv0")}, {}
-        nc.sync.dma_start(st_sb[:], st)
         w_raw = shared.tile([P, PACK, N], F32, name="w_raw", offset=place["w_raw"])
         nc.sync.dma_start(w_raw[:], w1.rearrange("(p j) m -> p j m", j=PACK))
+        nc.sync.dma_start(st_sb[:], st)
         word_table = shared.tile([P, T], I32, name="word_table", offset=place["word_table"])
         nc.sync.dma_start(word_table[:], x_words[0].rearrange("p n r -> p (n r)").bitcast(I32))
         picked_scales = keep.tile([P, S], U8, name="picked_scales")
@@ -67,157 +67,92 @@ def tile_picked_ppo8_none_p_kernel(tc, x_words, x_scales, w1, old, adv, offs, st
         for q in range(QUADRANTS):
             nc.sync.dma_start(x_scale[32 * q : 32 * q + 4, :], picked_scales[4 * q : 4 * q + 4, :].bitcast(I32))
 
-        ident = keep.tile([P, P], F32, name="ident")
-        make_identity(nc, ident[:])
-
         w_code, w_scale = [], []
-        a_sb, cap, plain = {}, {}, {}
-        turned, base, extra = {}, {}, {}
         blocks = [slice(b * P, (b + 1) * P) for b in range(S // P)]
+        whole = slice(0, S)
+        halves = [slice(0, S // 2), slice(S // 2, S)]
 
-        def gather_adv(t):
-            a_sb[t] = keep.tile([P, S], F32, name=f"a{t}")
-            nc.vector.tensor_copy(a_sb[t][:], adv_table[t][:].indirect(st_sb[:]))
+        def entries(lists, part):
+            return lists[:, part.start // 16 : part.stop // 16]
 
-        def quantize_weights(pair, casts):
+        def quantize_weights(pair, cast):
             grouped = keep.tile([P, PAIR, P, PACK], BF16, name=f"grouped{pair}", align_bytes=64)
             columns = w_raw[:].rearrange("p j (c t) -> p c t j", t=TILES)[:, :, pair * PAIR : (pair + 1) * PAIR, :]
-            for cast, tiles in casts:
-                cast(grouped[:, tiles].rearrange("p i c j -> p c i j"), columns[:, :, tiles, :])
+            cast(grouped[:].rearrange("p i c j -> p c i j"), columns)
             codes = keep.tile([P, PAIR * P], U32, name=f"w_code{pair}", align_bytes=64)
             scales = keep.tile([P, PAIR * P], U8, name=f"w_scale{pair}", align_bytes=64)
             nc.vector.quantize_mx(codes[:].bitcast(FP8X4), scales[:], grouped[:].rearrange("p i c j -> p (i c j)"))
             w_code.append(codes)
             w_scale.append(scales)
 
-        def project(t, parts, bank):
+        def project(t, part, bank):
             pair, i = divmod(t, PAIR)
             y_ps = psum.tile([P, S], F32, name="y_ps", tag=f"bank{bank}")
-            for part in parts:
-                nc.tensor.matmul_mx(
-                    y_ps[:, part],
-                    lhsT=w_code[pair][:, blocks[i]].bitcast(FP8X4),
-                    lhsT_scale=w_scale[pair][:, blocks[i]],
-                    rhs=x_code[:, part].bitcast(FP8X4),
-                    rhs_scale=x_scale[:].bitcast(U8)[:, part],
-                    start=True,
-                    stop=True,
-                )
+            nc.tensor.matmul_mx(
+                y_ps[:, part],
+                lhsT=w_code[pair][:, blocks[i]].bitcast(FP8X4),
+                lhsT_scale=w_scale[pair][:, blocks[i]],
+                rhs=x_code[:, part].bitcast(FP8X4),
+                rhs_scale=x_scale[:].bitcast(U8)[:, part],
+                start=True,
+                stop=True,
+            )
             return y_ps
 
-        def copy_y(y_ps, part, name):
-            y = keep.tile([P, part.stop - part.start], F32, name=name, tag=name)
-            nc.scalar.copy(y[:], y_ps[:, part])
-            return y
+        def gather(engine, picked, table, part):
+            looked_up = table[:].indirect(entries(st_sb, part))
+            if engine == "scalar":
+                nc.scalar.activation(picked[:, part], looked_up, ACT.Copy)
+            else:
+                nc.vector.tensor_copy(picked[:, part], looked_up)
 
-        def turn(t):
-            turned[t] = psum.tile([P, S], F32, name="turned", tag=f"bank{4 + t % 2}")
-            for block in blocks:
-                nc.tensor.transpose(turned[t][:, block], a_sb[t][:, block], ident[:])
-
-        def make_terms(t):
-            nc.scalar.activation(base[t][:, :], turned[t][:], ACT.Copy, scale=LOW)
-            nc.scalar.activation(extra[t][:, :], turned[t][:], ACT.Relu, scale=HIGH - LOW)
-
-        def make_cap(t):
-            cap[t] = psum.tile([P, S], F32, name="cap", tag=f"bank{(6, 7, 1, 2)[t]}")
-            passes = [(term, block) for term in (base[t], extra[t]) for block in blocks]
-            for n, (term, block) in enumerate(passes):
-                first, last = n == 0, n == len(passes) - 1
-                nc.tensor.matmul(cap[t][:, block], term[:, block], ident[:], start=first, stop=last, is_transpose=True)
-
-        def make_ratio(t, part, y):
-            entries = st_sb[:, part.start // 16 : part.stop // 16]
-            nc.vector.tensor_tensor(diff[t][:, part], old_table[t][:].indirect(entries), y, ALU.subtract)
-            nc.scalar.activation(ratio[t][:, part], diff[t][:, part], ACT.Exp, scale=-0.25)
-
-        def multiply(t):
-            nc.gpsimd.tensor_tensor(plain[t][:], ratio[t][:], a_sb[t][:], ALU.mult)
-
-        def multiply_last(part, product):
-            nc.vector.scalar_tensor_tensor(product, ratio[3][:, part], 1.0 / LOW, base_ps[:, part], ALU.mult, ALU.mult)
-
-        def finish(t, part, product):
-            nc.vector.tensor_tensor(result[t][:, part], product, cap[t][:, part], ALU.min)
-            nc.sync.dma_start(out_rows[:, t, part], result[t][:, part])
-
-        whole = slice(0, S)
-        halves = [slice(0, S // 2), slice(S // 2, S)]
-        diff = [keep.tile([P, S], F32, name=f"diff{t}", tag=f"diff{t}") for t in range(TILES)]
-        ratio = [keep.tile([P, S], F32, name=f"ratio{t}") for t in range(TILES)]
-
-        gather_adv(0)
-        turn(0)
-        adv_table[1] = load_table(adv_rows, 1, "adv1")
-        old_table[0] = load_table(old_rows, 0, "old0")
-        quantize_weights(0, [(nc.vector.tensor_copy, slice(0, 2))])
-        quantize_weights(1, [(nc.scalar.copy, slice(0, 2))])
+        old_table = {0: load_table(old_rows, 0, "old0")}
+        adv_table = {0: load_table(adv_rows, 0, "adv0")}
+        quantize_weights(0, nc.vector.tensor_copy)
+        quantize_weights(1, nc.scalar.copy)
         old_table[1] = load_table(old_rows, 1, "old1")
-        adv_table[2] = load_table(adv_rows, 2, "adv2")
-        base[0] = keep.tile([P, S], F32, name="base0")
-        extra[0] = keep.tile([P, S], F32, name="extra0")
-        make_terms(0)
-        make_cap(0)
+        adv_table[1] = load_table(adv_rows, 1, "adv1")
         x_code = keep.tile([P, S], U32, name="x_code", align_bytes=64)
         for part in halves:
-            entries = offs_sb[:, part.start // 16 : part.stop // 16]
-            nc.vector.tensor_copy(x_code[:, part], word_table[:].bitcast(U32).indirect(entries))
-        adv_table[3] = load_table(adv_rows, 3, "adv3")
+            nc.vector.tensor_copy(x_code[:, part], word_table[:].bitcast(U32).indirect(entries(offs_sb, part)))
         old_table[2] = load_table(old_rows, 2, "old2")
-        y0 = keep.tile([P, S], F32, name="y0", tag="y0")
-        y0_ps = [project(0, [part], h) for h, part in enumerate(halves)]
-        for part, y_ps in zip(halves, y0_ps):
-            nc.scalar.copy(y0[:, part], y_ps[:, part])
-        y1 = copy_y(project(1, [whole], 2), whole, "y1")
-        y2 = copy_y(project(2, [whole], 3), whole, "y2")[:]
-        y3_ps = project(3, [whole], 0)
-        gather_adv(1)
-        old_table[3] = load_table(old_rows, 3, "old3")
-        turn(1)
-        make_ratio(0, whole, y0[:])
-        make_ratio(1, whole, y1[:])
-        y_late = keep.tile([P, 2 * S + S // 2], F32, name="y_late", tag="diff0")
-        base[1], extra[1] = y_late[:, :S], y_late[:, S + S // 2 :]
-        make_terms(1)
-        y3_first = keep.tile([P, S // 2], F32, name="y3_first", tag="diff1")
-        y3 = [y3_first[:, :], y_late[:, S : S + S // 2]]
-        for part, y in zip(halves, y3):
-            nc.scalar.copy(y, y3_ps[:, part])
-        plain[0] = keep.tile([P, S], F32, name="plain0", tag="y1")
-        plain[1] = keep.tile([P, S], F32, name="plain1")
-        multiply(0)
-        multiply(1)
-        make_cap(1)
-        gather_adv(2)
-        gather_adv(3)
-        turn(2)
-        turn(3)
-        behind_adv = shared.tile([P, 3, S], F32, name="behind_adv", offset=place["behind_adv"])
-        base[2], extra[2] = behind_adv[:, 0, :], behind_adv[:, 1, :]
-        result = {0: behind_adv[:, 2, :]}
-        finish(0, whole, plain[0][:])
-        base[3] = keep.tile([P, S], F32, name="base3")
-        extra[3] = keep.tile([P, S], F32, name="extra3")
-        make_terms(2)
-        make_terms(3)
-        make_ratio(2, whole, y2)
-        for part, y in zip(halves, y3):
-            make_ratio(3, part, y)
-        result[1] = keep.tile([P, S], F32, name="result1", tag="diff1")
-        plain[2] = keep.tile([P, S], F32, name="plain2", tag="diff0")
-        last = [keep.tile([P, S // 2], F32, name=f"plain3_{h}", tag=f"plain3_{h}") for h in range(2)]
-        result[3] = keep.tile([P, S], F32, name="result3")
-        multiply(2)
-        make_cap(2)
-        base_ps = psum.tile([P, S], F32, name="base_ps", tag="bank3")
-        for block in blocks:
-            nc.tensor.transpose(base_ps[:, block], base[3][:, block], ident[:])
-        make_cap(3)
-        finish(1, whole, plain[1][:])
-        for part, product in zip(halves, last):
-            multiply_last(part, product[:])
-        for part, product in zip(halves, last):
-            finish(3, part, product[:])
-        result[2] = keep.tile([P, S], F32, name="result2", tag="plain3_0")
-        for part in halves:
-            finish(2, part, plain[2][:, part])
+        adv_table[2] = load_table(adv_rows, 2, "adv2")
+        y = {0: [project(0, part, h) for h, part in enumerate(halves)]}
+        for t in range(1, TILES):
+            y[t] = [project(t, whole, t + 1)] * 2
+
+        for t in range(TILES):
+            if t == 0:
+                picked_old = shared.tile([P, S], F32, name="picked_old0", offset=place["picked_old0"])
+            else:
+                picked_old = keep.tile([P, S], F32, name=f"picked_old{t}")
+            a = keep.tile([P, S], F32, name=f"a{t}")
+            diff = keep.tile([P, S], F32, name=f"diff{t}")
+            cap = keep.tile([P, S], F32, name=f"cap{t}")
+            plain = keep.tile([P, S], F32, name=f"plain{t}")
+            result = keep.tile([P, S], F32, name=f"result{t}")
+            if t == 0:
+                for engine, part in zip(("scalar", "vector"), halves):
+                    gather(engine, picked_old, old_table[t], part)
+                old_table[3] = load_table(old_rows, 3, "old3")
+                for part, y_ps in zip(halves, y[t]):
+                    nc.vector.tensor_tensor(diff[:, part], picked_old[:, part], y_ps[:, part], ALU.subtract)
+                adv_table[3] = load_table(adv_rows, 3, "adv3")
+            else:
+                gather("scalar", picked_old, old_table[t], whole)
+                nc.vector.tensor_tensor(diff[:], picked_old[:], y[t][0][:], ALU.subtract)
+            if t < 1:
+                for engine, part in zip(("scalar", "vector"), halves):
+                    gather(engine, a, adv_table[t], part)
+            else:
+                gather("scalar", a, adv_table[t], whole)
+            ratio = keep.tile([P, S], F32, name=f"ratio{t}")
+            parts = halves if t == TILES - 1 else [whole]
+            for part in parts:
+                nc.scalar.activation(ratio[:, part], diff[:, part], ACT.Exp, scale=-0.25)
+            nc.vector.scalar_tensor_tensor(cap[:], a[:], HIGH / LOW, a[:], ALU.mult, ALU.max)
+            for part in parts:
+                nc.vector.tensor_tensor(plain[:, part], ratio[:, part], a[:, part], ALU.mult)
+            for part in parts:
+                nc.vector.scalar_tensor_tensor(result[:, part], cap[:, part], LOW, plain[:, part], ALU.mult, ALU.min)
+                nc.sync.dma_start(out_rows[:, t, part], result[:, part])

@@ -33,11 +33,13 @@ def tile_picked_ppo8_none_p_kernel(tc, x_words, x_scales, w1, old, adv, offs, st
         st_sb = keep.tile([P, S // 16], U16, name="st_sb")
         shared = ctx.enter_context(tc.tile_pool(name="shared", bufs=1))
         place = {
-            "scale_table": 3 * TABLE // 4, "old0": 0, "adv0": TABLE, "ratio0": TABLE,
-            "w_raw": 2 * TABLE, "old1": 2 * TABLE, "adv1": 3 * TABLE, "ratio1": 3 * TABLE,
-            "word_table": 4 * TABLE, "old2": 4 * TABLE, "adv2": 5 * TABLE, "ratio2": 5 * TABLE,
-            "old3": 0, "adv3": 6 * TABLE, "ratio3": 6 * TABLE, "picked_old0": 6 * TABLE,
+            "scale_table": 3 * TABLE // 4, "old0": 0, "adv0": TABLE,
+            "w_raw": 2 * TABLE, "old1": 2 * TABLE, "adv1": 3 * TABLE,
+            "word_table": 4 * TABLE, "old2": 4 * TABLE, "adv2": 5 * TABLE,
+            "old3": 0, "adv3": 6 * TABLE, "picked_old0_0": 6 * TABLE,
         }
+        for t in range(1, TILES):
+            place[f"picked_old{t}_0"] = place[f"result{t - 1}"] = (6 + t) * TABLE
 
         scale_table = shared.tile([P, T // 4], I32, name="scale_table", offset=place["scale_table"])
         nc.gpsimd.memset(scale_table[:], 0)
@@ -102,9 +104,9 @@ def tile_picked_ppo8_none_p_kernel(tc, x_words, x_scales, w1, old, adv, offs, st
         def gather(engine, picked, table, part):
             looked_up = table[:].indirect(entries(st_sb, part))
             if engine == "scalar":
-                nc.scalar.activation(picked[:, part], looked_up, ACT.Copy)
+                nc.scalar.activation(picked, looked_up, ACT.Copy)
             else:
-                nc.vector.tensor_copy(picked[:, part], looked_up)
+                nc.vector.tensor_copy(picked, looked_up)
 
         old_table = {0: load_table(old_rows, 0, "old0")}
         adv_table = {0: load_table(adv_rows, 0, "adv0")}
@@ -121,38 +123,76 @@ def tile_picked_ppo8_none_p_kernel(tc, x_words, x_scales, w1, old, adv, offs, st
         for t in range(1, TILES):
             y[t] = [project(t, whole, t + 1)] * 2
 
-        for t in range(TILES):
-            if t == 0:
-                picked_old = shared.tile([P, S], F32, name="picked_old0", offset=place["picked_old0"])
-            else:
-                picked_old = keep.tile([P, S], F32, name=f"picked_old{t}")
-            a = keep.tile([P, S], F32, name=f"a{t}")
-            diff = keep.tile([P, S], F32, name=f"diff{t}")
-            cap = keep.tile([P, S], F32, name=f"cap{t}")
-            plain = keep.tile([P, S], F32, name=f"plain{t}")
-            result = keep.tile([P, S], F32, name=f"result{t}")
-            if t == 0:
-                for engine, part in zip(("scalar", "vector"), halves):
-                    gather(engine, picked_old, old_table[t], part)
-                old_table[3] = load_table(old_rows, 3, "old3")
-                for part, y_ps in zip(halves, y[t]):
-                    nc.vector.tensor_tensor(diff[:, part], picked_old[:, part], y_ps[:, part], ALU.subtract)
-                adv_table[3] = load_table(adv_rows, 3, "adv3")
-            else:
-                gather("scalar", picked_old, old_table[t], whole)
-                nc.vector.tensor_tensor(diff[:], picked_old[:], y[t][0][:], ALU.subtract)
-            if t < 1:
-                for engine, part in zip(("scalar", "vector"), halves):
-                    gather(engine, a, adv_table[t], part)
-            else:
-                gather("scalar", a, adv_table[t], whole)
-            ratio = keep.tile([P, S], F32, name=f"ratio{t}")
-            parts = halves if t == TILES - 1 else [whole]
+        def new(name, width=S):
+            if name in place:
+                return shared.tile([P, width], F32, name=name, offset=place[name])
+            return keep.tile([P, width], F32, name=name)
+
+        picked_old, a, diff, ratio, cap, plain = {}, {}, {}, {}, {}, {}
+
+        def gather_old(t, engines):
+            picked_old[t] = [new(f"picked_old{t}_{h}", S // 2) for h in range(2)]
+            for engine, picked, part in zip(engines, picked_old[t], halves):
+                gather(engine, picked[:], old_table[t], part)
+
+        def subtract(t):
+            diff[t] = new(f"diff{t}")
+            for h, part in enumerate(halves):
+                nc.vector.tensor_tensor(diff[t][:, part], picked_old[t][h][:], y[t][h][:, part], ALU.subtract)
+
+        def gather_adv(t, engine, part):
+            if t not in a:
+                a[t] = new(f"a{t}")
+            gather(engine, a[t][:, part], adv_table[t], part)
+
+        def exponential(t, part):
+            if t not in ratio:
+                ratio[t] = new(f"ratio{t}")
+            nc.scalar.activation(ratio[t][:, part], diff[t][:, part], ACT.Exp, scale=-0.25)
+
+        def make_cap(t, part):
+            if t not in cap:
+                cap[t] = new(f"cap{t}")
+            nc.vector.scalar_tensor_tensor(cap[t][:, part], a[t][:, part], HIGH / LOW, a[t][:, part], ALU.mult, ALU.max)
+
+        def multiply(t, part):
+            if t not in plain:
+                plain[t] = new(f"plain{t}")
+            nc.vector.tensor_tensor(plain[t][:, part], ratio[t][:, part], a[t][:, part], ALU.mult)
+
+        def finish(t, parts):
+            result = new(f"result{t}")
             for part in parts:
-                nc.scalar.activation(ratio[:, part], diff[:, part], ACT.Exp, scale=-0.25)
-            nc.vector.scalar_tensor_tensor(cap[:], a[:], HIGH / LOW, a[:], ALU.mult, ALU.max)
-            for part in parts:
-                nc.vector.tensor_tensor(plain[:, part], ratio[:, part], a[:, part], ALU.mult)
-            for part in parts:
-                nc.vector.scalar_tensor_tensor(result[:, part], cap[:, part], LOW, plain[:, part], ALU.mult, ALU.min)
+                nc.vector.scalar_tensor_tensor(result[:, part], cap[t][:, part], LOW, plain[t][:, part], ALU.mult, ALU.min)
                 nc.sync.dma_start(out_rows[:, t, part], result[:, part])
+
+        for t in range(TILES):
+            last = t == TILES - 1
+            gather_old(t, ("scalar", "vector") if t == 0 else ("scalar", "scalar"))
+            if t == 0:
+                old_table[3] = load_table(old_rows, 3, "old3")
+            subtract(t)
+            if t == 0:
+                adv_table[3] = load_table(adv_rows, 3, "adv3")
+            if t < 2:
+                gather_adv(t, "scalar", halves[0])
+                gather_adv(t, "vector", halves[1])
+                exponential(t, whole)
+            elif not last:
+                gather_adv(t, "scalar", whole)
+                exponential(t, whole)
+            else:
+                for part in halves:
+                    gather_adv(t, "scalar", part)
+                    exponential(t, part)
+            if t > 0:
+                finish(t - 1, [whole])
+            if t == 0:
+                for part in halves:
+                    make_cap(t, part)
+                multiply(t, whole)
+            else:
+                for part in halves if last else [whole]:
+                    make_cap(t, part)
+                    multiply(t, part)
+        finish(TILES - 1, halves)

@@ -36,10 +36,9 @@ def tile_picked_ppo8_none_p_kernel(tc, x_words, x_scales, w1, old, adv, offs, st
             "scale_table": 3 * TABLE // 4, "old0": 0, "adv0": TABLE,
             "w_raw": 2 * TABLE, "old1": 2 * TABLE, "adv1": 3 * TABLE,
             "word_table": 4 * TABLE, "old2": 4 * TABLE, "adv2": 5 * TABLE,
-            "old3": 0, "adv3": 6 * TABLE, "picked_old0_0": 6 * TABLE,
+            "diff0_256": 0, "old3": 0, "adv3": TABLE,
+            "plain0": 2 * TABLE, "result0": 3 * TABLE, "result1": 4 * TABLE, "result2": 0,
         }
-        for t in range(1, TILES):
-            place[f"picked_old{t}_0"] = place[f"result{t - 1}"] = (6 + t) * TABLE
 
         scale_table = shared.tile([P, T // 4], I32, name="scale_table", offset=place["scale_table"])
         nc.gpsimd.memset(scale_table[:], 0)
@@ -130,25 +129,25 @@ def tile_picked_ppo8_none_p_kernel(tc, x_words, x_scales, w1, old, adv, offs, st
 
         picked_old, a, diff, ratio, cap, plain = {}, {}, {}, {}, {}, {}
 
-        def gather_old(t, engines):
-            picked_old[t] = [new(f"picked_old{t}_{h}", S // 2) for h in range(2)]
-            for engine, picked, part in zip(engines, picked_old[t], halves):
-                gather(engine, picked[:], old_table[t], part)
+        def gather_old(t, engine, part):
+            if t not in picked_old:
+                picked_old[t] = new(f"picked_old{t}")
+            gather(engine, picked_old[t][:, part], old_table[t], part)
 
-        def subtract(t):
-            diff[t] = new(f"diff{t}")
-            for h, part in enumerate(halves):
-                nc.vector.tensor_tensor(diff[t][:, part], picked_old[t][h][:], y[t][h][:, part], ALU.subtract)
+        def subtract(t, part):
+            diff[t, part.start] = new(f"diff{t}_{part.start}", part.stop - part.start)
+            y_ps = y[t][part.start // (S // 2)]
+            nc.vector.tensor_tensor(diff[t, part.start][:], picked_old[t][:, part], y_ps[:, part], ALU.subtract)
 
         def gather_adv(t, engine, part):
             if t not in a:
                 a[t] = new(f"a{t}")
             gather(engine, a[t][:, part], adv_table[t], part)
 
-        def exponential(t, part):
+        def exponential(t, part, difference):
             if t not in ratio:
                 ratio[t] = new(f"ratio{t}")
-            nc.scalar.activation(ratio[t][:, part], diff[t][:, part], ACT.Exp, scale=-0.25)
+            nc.scalar.activation(ratio[t][:, part], difference, ACT.Exp, scale=-0.25)
 
         def make_cap(t, part):
             if t not in cap:
@@ -166,33 +165,30 @@ def tile_picked_ppo8_none_p_kernel(tc, x_words, x_scales, w1, old, adv, offs, st
                 nc.vector.scalar_tensor_tensor(result[:, part], cap[t][:, part], LOW, plain[t][:, part], ALU.mult, ALU.min)
                 nc.sync.dma_start(out_rows[:, t, part], result[:, part])
 
-        for t in range(TILES):
+        gather_old(0, "scalar", halves[0])
+        gather_old(0, "vector", halves[1])
+        for part in halves:
+            subtract(0, part)
+        for part in halves:
+            exponential(0, part, diff[0, part.start][:])
+        old_table[3] = load_table(old_rows, 3, "old3")
+        gather_adv(0, "vector", whole)
+        adv_table[3] = load_table(adv_rows, 3, "adv3")
+        make_cap(0, whole)
+        for t in range(1, TILES):
             last = t == TILES - 1
-            gather_old(t, ("scalar", "vector") if t == 0 else ("scalar", "scalar"))
-            if t == 0:
-                old_table[3] = load_table(old_rows, 3, "old3")
-            subtract(t)
-            if t == 0:
-                adv_table[3] = load_table(adv_rows, 3, "adv3")
-            if t < 2:
-                gather_adv(t, "scalar", halves[0])
-                gather_adv(t, "vector", halves[1])
-                exponential(t, whole)
-            elif not last:
-                gather_adv(t, "scalar", whole)
-                exponential(t, whole)
+            gather_old(t, "scalar", whole)
+            subtract(t, whole)
+            if t == 1:
+                multiply(0, whole)
             else:
-                for part in halves:
-                    gather_adv(t, "scalar", part)
-                    exponential(t, part)
-            if t > 0:
                 finish(t - 1, [whole])
-            if t == 0:
-                for part in halves:
-                    make_cap(t, part)
-                multiply(t, whole)
-            else:
-                for part in halves if last else [whole]:
-                    make_cap(t, part)
-                    multiply(t, part)
+            gather_adv(t, "scalar", whole)
+            for part in halves if last else [whole]:
+                exponential(t, part, diff[t, 0][:, part])
+            make_cap(t, whole)
+            if t == 1:
+                finish(0, [whole])
+            for part in halves if last else [whole]:
+                multiply(t, part)
         finish(TILES - 1, halves)

@@ -37,7 +37,7 @@ def tile_picked_ppo8_none_p_kernel(tc, x_words, x_scales, w1, old, adv, offs, st
             "w_raw": 2 * TABLE, "old1": 2 * TABLE, "adv1": 3 * TABLE,
             "word_table": 4 * TABLE, "old2": 4 * TABLE, "adv2": 5 * TABLE,
             "diff0_256": 0, "old3": 0, "adv3": TABLE,
-            "plain0": 2 * TABLE, "result0": 3 * TABLE, "result1": 4 * TABLE, "result2": 0,
+            "plain0": 2 * TABLE, "result0": 3 * TABLE, "result1": 4 * TABLE,
         }
 
         scale_table = shared.tile([P, T // 4], I32, name="scale_table", offset=place["scale_table"])
@@ -119,7 +119,7 @@ def tile_picked_ppo8_none_p_kernel(tc, x_words, x_scales, w1, old, adv, offs, st
         old_table[2] = load_table(old_rows, 2, "old2")
         adv_table[2] = load_table(adv_rows, 2, "adv2")
         y = {0: [project(0, part, h) for h, part in enumerate(halves)]}
-        for t in range(1, TILES):
+        for t in reversed(range(1, TILES)):
             y[t] = [project(t, whole, t + 1)] * 2
 
         def new(name, width=S):
@@ -183,10 +183,12 @@ def tile_picked_ppo8_none_p_kernel(tc, x_words, x_scales, w1, old, adv, offs, st
                 multiply(0, whole)
             else:
                 finish(t - 1, [whole])
-            gather_adv(t, "scalar", whole)
+            for part in halves if last else [whole]:
+                gather_adv(t, "scalar", part)
             for part in halves if last else [whole]:
                 exponential(t, part, diff[t, 0][:, part])
-            make_cap(t, whole)
+            for part in halves if last else [whole]:
+                make_cap(t, part)
             if t == 1:
                 finish(0, [whole])
             for part in halves if last else [whole]:

@@ -36,8 +36,10 @@ def tile_picked_ppo8_none_p_kernel(tc, x_words, x_scales, w1, old, adv, offs, st
             "scale_table": 3 * TABLE // 4, "old0": 0, "adv0": TABLE,
             "w_raw": 2 * TABLE, "old1": 2 * TABLE, "adv1": 3 * TABLE,
             "word_table": 4 * TABLE, "old2": 4 * TABLE, "adv2": 5 * TABLE,
-            "diff0_256": 0, "old3": 0, "adv3": TABLE,
-            "plain0": 2 * TABLE, "result0": 3 * TABLE, "result1": 4 * TABLE,
+            "diff0_256": 0, "old3": 0, "adv3": 6 * TABLE, "ratio0": 6 * TABLE, "picked_old0": 6 * TABLE,
+            "picked_old2": 7 * TABLE, "ratio2": 7 * TABLE,
+            "result0": 2 * TABLE, "diff2_256": 4 * TABLE, "plain1": 4 * TABLE + TABLE // 4,
+            "result1": 5 * TABLE, "result2": 0,
         }
 
         scale_table = shared.tile([P, T // 4], I32, name="scale_table", offset=place["scale_table"])
@@ -169,28 +171,41 @@ def tile_picked_ppo8_none_p_kernel(tc, x_words, x_scales, w1, old, adv, offs, st
         gather_old(0, "vector", halves[1])
         for part in halves:
             subtract(0, part)
+        gather_adv(0, "scalar", halves[0])
+        gather_adv(0, "vector", halves[1])
         for part in halves:
             exponential(0, part, diff[0, part.start][:])
         old_table[3] = load_table(old_rows, 3, "old3")
-        gather_adv(0, "vector", whole)
         adv_table[3] = load_table(adv_rows, 3, "adv3")
         make_cap(0, whole)
-        for t in range(1, TILES):
-            last = t == TILES - 1
-            gather_old(t, "scalar", whole)
-            subtract(t, whole)
-            if t == 1:
-                multiply(0, whole)
-            else:
-                finish(t - 1, [whole])
-            for part in halves if last else [whole]:
-                gather_adv(t, "scalar", part)
-            for part in halves if last else [whole]:
-                exponential(t, part, diff[t, 0][:, part])
-            for part in halves if last else [whole]:
-                make_cap(t, part)
-            if t == 1:
-                finish(0, [whole])
-            for part in halves if last else [whole]:
-                multiply(t, part)
-        finish(TILES - 1, halves)
+        multiply(0, whole)
+
+        gather_old(1, "scalar", whole)
+        subtract(1, whole)
+        finish(0, [whole])
+        gather_adv(1, "scalar", whole)
+        exponential(1, whole, diff[1, 0][:])
+        make_cap(1, whole)
+
+        gather_old(2, "scalar", halves[0])
+        gather_old(2, "vector", halves[1])
+        for part in halves:
+            subtract(2, part)
+        multiply(1, whole)
+        gather_adv(2, "scalar", whole)
+        for part in halves:
+            exponential(2, part, diff[2, part.start][:])
+        make_cap(2, whole)
+        finish(1, [whole])
+        multiply(2, whole)
+
+        gather_old(3, "scalar", whole)
+        subtract(3, whole)
+        finish(2, [whole])
+        gather_adv(3, "scalar", whole)
+        for part in halves:
+            exponential(3, part, diff[3, 0][:, part])
+        make_cap(3, whole)
+        for part in halves:
+            multiply(3, part)
+        finish(3, halves)

@@ -38,8 +38,8 @@ def tile_picked_ppo8_none_p_kernel(tc, x_words, x_scales, w1, old, adv, offs, st
             "word_table": 4 * TABLE, "old2": 4 * TABLE, "adv2": 5 * TABLE,
             "diff0_256": 0, "old3": 0, "adv3": 6 * TABLE, "ratio0": 6 * TABLE, "picked_old0": 6 * TABLE,
             "picked_old2": 7 * TABLE, "ratio2": 7 * TABLE,
-            "result0": 2 * TABLE, "diff2_256": 4 * TABLE, "plain1": 4 * TABLE + TABLE // 4,
-            "result1": 5 * TABLE, "result2": 0,
+            "result0": 2 * TABLE, "diff2_256": 4 * TABLE, "result1": 4 * TABLE + TABLE // 4,
+            "result2": 0,
         }
 
         scale_table = shared.tile([P, T // 4], I32, name="scale_table", offset=place["scale_table"])
@@ -186,17 +186,18 @@ def tile_picked_ppo8_none_p_kernel(tc, x_words, x_scales, w1, old, adv, offs, st
         gather_adv(1, "scalar", whole)
         exponential(1, whole, diff[1, 0][:])
         make_cap(1, whole)
+        plain[1] = new("plain1")
+        nc.gpsimd.tensor_tensor(plain[1][:], ratio[1][:], a[1][:], ALU.mult)
 
         gather_old(2, "scalar", halves[0])
         gather_old(2, "vector", halves[1])
         for part in halves:
             subtract(2, part)
-        multiply(1, whole)
+        finish(1, [whole])
         gather_adv(2, "scalar", whole)
         for part in halves:
             exponential(2, part, diff[2, part.start][:])
         make_cap(2, whole)
-        finish(1, [whole])
         multiply(2, whole)
 
         gather_old(3, "scalar", whole)

@@ -37,9 +37,10 @@ def tile_picked_ppo8_none_p_kernel(tc, x_words, x_scales, w1, old, adv, offs, st
             "w_raw": 2 * TABLE, "old1": 2 * TABLE, "adv1": 3 * TABLE,
             "word_table": 4 * TABLE, "old2": 4 * TABLE, "adv2": 5 * TABLE,
             "diff0_256": 0, "old3": 0, "adv3": 6 * TABLE, "ratio0": 6 * TABLE, "picked_old0": 6 * TABLE,
-            "picked_old2": 7 * TABLE, "ratio2": 7 * TABLE,
-            "result0": 2 * TABLE, "diff2_256": 4 * TABLE, "result1": 4 * TABLE + TABLE // 4,
-            "result2": 0,
+            "diff1_256": 2 * TABLE, "cap0": 2 * TABLE + TABLE // 4,
+            "diff2_256": 4 * TABLE, "result0": 4 * TABLE + TABLE // 4,
+            "picked_old1": 8 * TABLE, "ratio1": 8 * TABLE, "picked_old2": 7 * TABLE, "ratio2": 7 * TABLE,
+            "result1": 5 * TABLE, "result2": 0,
         }
 
         scale_table = shared.tile([P, T // 4], I32, name="scale_table", offset=place["scale_table"])
@@ -156,10 +157,10 @@ def tile_picked_ppo8_none_p_kernel(tc, x_words, x_scales, w1, old, adv, offs, st
                 cap[t] = new(f"cap{t}")
             nc.vector.scalar_tensor_tensor(cap[t][:, part], a[t][:, part], HIGH / LOW, a[t][:, part], ALU.mult, ALU.max)
 
-        def multiply(t, part):
+        def multiply(t, part, engine=nc.vector):
             if t not in plain:
                 plain[t] = new(f"plain{t}")
-            nc.vector.tensor_tensor(plain[t][:, part], ratio[t][:, part], a[t][:, part], ALU.mult)
+            engine.tensor_tensor(plain[t][:, part], ratio[t][:, part], a[t][:, part], ALU.mult)
 
         def finish(t, parts):
             result = new(f"result{t}")
@@ -176,28 +177,30 @@ def tile_picked_ppo8_none_p_kernel(tc, x_words, x_scales, w1, old, adv, offs, st
         for part in halves:
             exponential(0, part, diff[0, part.start][:])
         old_table[3] = load_table(old_rows, 3, "old3")
+        multiply(0, whole, nc.gpsimd)
         adv_table[3] = load_table(adv_rows, 3, "adv3")
-        make_cap(0, whole)
-        multiply(0, whole)
 
-        gather_old(1, "scalar", whole)
-        subtract(1, whole)
-        finish(0, [whole])
+        gather_old(1, "scalar", halves[0])
+        gather_old(1, "vector", halves[1])
+        for part in halves:
+            subtract(1, part)
+        make_cap(0, whole)
         gather_adv(1, "scalar", whole)
-        exponential(1, whole, diff[1, 0][:])
+        for part in halves:
+            exponential(1, part, diff[1, part.start][:])
         make_cap(1, whole)
-        plain[1] = new("plain1")
-        nc.gpsimd.tensor_tensor(plain[1][:], ratio[1][:], a[1][:], ALU.mult)
+        multiply(1, whole, nc.gpsimd)
 
         gather_old(2, "scalar", halves[0])
         gather_old(2, "vector", halves[1])
         for part in halves:
             subtract(2, part)
-        finish(1, [whole])
+        finish(0, [whole])
         gather_adv(2, "scalar", whole)
         for part in halves:
             exponential(2, part, diff[2, part.start][:])
         make_cap(2, whole)
+        finish(1, [whole])
         multiply(2, whole)
 
         gather_old(3, "scalar", whole)

@@ -40,7 +40,8 @@ def tile_picked_ppo8_none_p_kernel(tc, x_words, x_scales, w1, old, adv, offs, st
             "diff1_256": 2 * TABLE, "cap0": 2 * TABLE + TABLE // 4,
             "diff2_256": 4 * TABLE, "result0": 4 * TABLE + TABLE // 4,
             "picked_old1": 8 * TABLE, "ratio1": 8 * TABLE, "picked_old2": 7 * TABLE, "ratio2": 7 * TABLE,
-            "result1": 5 * TABLE, "result2": 0,
+            "diff3_256": 0, "result1": TABLE // 4, "picked_old3": 9 * TABLE, "ratio3": 9 * TABLE,
+            "plain0": 10 * TABLE, "plain2": 10 * TABLE, "result2": 6 * TABLE,
         }
 
         scale_table = shared.tile([P, T // 4], I32, name="scale_table", offset=place["scale_table"])
@@ -200,16 +201,18 @@ def tile_picked_ppo8_none_p_kernel(tc, x_words, x_scales, w1, old, adv, offs, st
         for part in halves:
             exponential(2, part, diff[2, part.start][:])
         make_cap(2, whole)
-        finish(1, [whole])
-        multiply(2, whole)
+        multiply(2, whole, nc.gpsimd)
 
-        gather_old(3, "scalar", whole)
-        subtract(3, whole)
-        finish(2, [whole])
+        gather_old(3, "scalar", halves[0])
+        gather_old(3, "vector", halves[1])
+        for part in halves:
+            subtract(3, part)
+        finish(1, [whole])
         gather_adv(3, "scalar", whole)
         for part in halves:
-            exponential(3, part, diff[3, 0][:, part])
+            exponential(3, part, diff[3, part.start][:])
         make_cap(3, whole)
+        finish(2, [whole])
         for part in halves:
             multiply(3, part)
         finish(3, halves)

@@ -22,6 +22,7 @@ TILES = N // P
 PAIR = 2
 LOW, HIGH = 0.8, 1.25
 TABLE = 4 * U
+NEAR = 128
 
 
 def tile_picked_ppo8_none_p_kernel(tc, x_words, x_scales, w1, old, adv, offs, st, out):
@@ -36,13 +37,15 @@ def tile_picked_ppo8_none_p_kernel(tc, x_words, x_scales, w1, old, adv, offs, st
             "scale_table": 3 * TABLE // 4, "old0": 0, "adv0": TABLE,
             "w_raw": 2 * TABLE, "old1": 2 * TABLE, "adv1": 3 * TABLE,
             "word_table": 4 * TABLE, "old2": 4 * TABLE, "adv2": 5 * TABLE,
-            "diff0_256": 0, "old3": 0, "adv3": 6 * TABLE, "ratio0": 6 * TABLE, "picked_old0": 6 * TABLE,
-            "diff1_256": 2 * TABLE, "cap0": 2 * TABLE + TABLE // 4,
-            "diff2_256": 4 * TABLE, "result0": 4 * TABLE + TABLE // 4,
-            "picked_old1": 8 * TABLE, "ratio1": 8 * TABLE, "picked_old2": 7 * TABLE, "ratio2": 7 * TABLE,
-            "diff3_256": 0, "result1": TABLE // 4, "picked_old3": 9 * TABLE, "ratio3": 9 * TABLE,
-            "plain0": 10 * TABLE, "plain2": 10 * TABLE, "result2": 6 * TABLE,
+            "old3": 0, "adv3": 6 * TABLE,
         }
+        for t in range(TILES):
+            place[f"diff{t}_256"] = place[f"old{t}"]
+            place[f"picked_old{t}"] = place[f"ratio{t}"] = (6 + t) * TABLE
+            place[f"plain{t}_{NEAR}"] = 10 * TABLE
+            if t:
+                place[f"plain{t - 1}_0"] = place[f"old{t}"] + TABLE // 4
+                place[f"result{t - 1}"] = place[f"old{t}"] + TABLE // 2
 
         scale_table = shared.tile([P, T // 4], I32, name="scale_table", offset=place["scale_table"])
         nc.gpsimd.memset(scale_table[:], 0)
@@ -132,87 +135,61 @@ def tile_picked_ppo8_none_p_kernel(tc, x_words, x_scales, w1, old, adv, offs, st
             return keep.tile([P, width], F32, name=name)
 
         picked_old, a, diff, ratio, cap, plain = {}, {}, {}, {}, {}, {}
+        near, far = slice(0, NEAR), slice(NEAR, S)
 
-        def gather_old(t, engine, part):
-            if t not in picked_old:
-                picked_old[t] = new(f"picked_old{t}")
-            gather(engine, picked_old[t][:, part], old_table[t], part)
+        def gather_old(t):
+            picked_old[t] = new(f"picked_old{t}")
+            for engine, part in zip(("scalar", "vector"), halves):
+                gather(engine, picked_old[t][:, part], old_table[t], part)
 
-        def subtract(t, part):
-            diff[t, part.start] = new(f"diff{t}_{part.start}", part.stop - part.start)
-            y_ps = y[t][part.start // (S // 2)]
-            nc.vector.tensor_tensor(diff[t, part.start][:], picked_old[t][:, part], y_ps[:, part], ALU.subtract)
+        def subtract(t):
+            for h, part in enumerate(halves):
+                diff[t, h] = new(f"diff{t}_{part.start}", S // 2)
+                nc.vector.tensor_tensor(diff[t, h][:], picked_old[t][:, part], y[t][h][:, part], ALU.subtract)
 
-        def gather_adv(t, engine, part):
-            if t not in a:
-                a[t] = new(f"a{t}")
-            gather(engine, a[t][:, part], adv_table[t], part)
+        def gather_adv(t, shares):
+            a[t] = new(f"a{t}")
+            for engine, part in shares:
+                gather(engine, a[t][:, part], adv_table[t], part)
 
-        def exponential(t, part, difference):
-            if t not in ratio:
-                ratio[t] = new(f"ratio{t}")
-            nc.scalar.activation(ratio[t][:, part], difference, ACT.Exp, scale=-0.25)
+        def exponential(t):
+            ratio[t] = new(f"ratio{t}")
+            for h, part in enumerate(halves):
+                nc.scalar.activation(ratio[t][:, part], diff[t, h][:], ACT.Exp, scale=-0.25)
 
-        def make_cap(t, part):
-            if t not in cap:
-                cap[t] = new(f"cap{t}")
-            nc.vector.scalar_tensor_tensor(cap[t][:, part], a[t][:, part], HIGH / LOW, a[t][:, part], ALU.mult, ALU.max)
+        def make_cap(t):
+            cap[t] = new(f"cap{t}")
+            nc.vector.scalar_tensor_tensor(cap[t][:], a[t][:], HIGH / LOW, a[t][:], ALU.mult, ALU.max)
 
-        def multiply(t, part, engine=nc.vector):
-            if t not in plain:
-                plain[t] = new(f"plain{t}")
-            engine.tensor_tensor(plain[t][:, part], ratio[t][:, part], a[t][:, part], ALU.mult)
+        def multiply(t, part, engine):
+            plain[t, part.start] = new(f"plain{t}_{part.start}", part.stop - part.start)
+            engine.tensor_tensor(plain[t, part.start][:], ratio[t][:, part], a[t][:, part], ALU.mult)
 
-        def finish(t, parts):
-            result = new(f"result{t}")
-            for part in parts:
-                nc.vector.scalar_tensor_tensor(result[:, part], cap[t][:, part], LOW, plain[t][:, part], ALU.mult, ALU.min)
-                nc.sync.dma_start(out_rows[:, t, part], result[:, part])
+        def minimum(t, result, part):
+            nc.vector.scalar_tensor_tensor(result[:, part], cap[t][:, part], LOW, plain[t, part.start][:], ALU.mult, ALU.min)
 
-        gather_old(0, "scalar", halves[0])
-        gather_old(0, "vector", halves[1])
+        last = TILES - 1
+        for t in range(TILES):
+            gather_old(t)
+            subtract(t)
+            if t:
+                multiply(t - 1, near, nc.vector)
+                if t == 1:
+                    adv_table[last] = load_table(adv_rows, last, f"adv{last}")
+                result = new(f"result{t - 1}")
+                for part in (far, near):
+                    minimum(t - 1, result, part)
+                nc.sync.dma_start(out_rows[:, t - 1, :], result[:])
+            gather_adv(t, [("scalar", whole)] if t else zip(("scalar", "vector"), halves))
+            exponential(t)
+            make_cap(t)
+            if t == 0:
+                old_table[last] = load_table(old_rows, last, f"old{last}")
+            if t < last:
+                multiply(t, far, nc.gpsimd)
         for part in halves:
-            subtract(0, part)
-        gather_adv(0, "scalar", halves[0])
-        gather_adv(0, "vector", halves[1])
+            multiply(last, part, nc.vector)
+        result = new(f"result{last}")
         for part in halves:
-            exponential(0, part, diff[0, part.start][:])
-        old_table[3] = load_table(old_rows, 3, "old3")
-        multiply(0, whole, nc.gpsimd)
-        adv_table[3] = load_table(adv_rows, 3, "adv3")
-
-        gather_old(1, "scalar", halves[0])
-        gather_old(1, "vector", halves[1])
-        for part in halves:
-            subtract(1, part)
-        make_cap(0, whole)
-        gather_adv(1, "scalar", whole)
-        for part in halves:
-            exponential(1, part, diff[1, part.start][:])
-        make_cap(1, whole)
-        multiply(1, whole, nc.gpsimd)
-
-        gather_old(2, "scalar", halves[0])
-        gather_old(2, "vector", halves[1])
-        for part in halves:
-            subtract(2, part)
-        finish(0, [whole])
-        gather_adv(2, "scalar", whole)
-        for part in halves:
-            exponential(2, part, diff[2, part.start][:])
-        make_cap(2, whole)
-        multiply(2, whole, nc.gpsimd)
-
-        gather_old(3, "scalar", halves[0])
-        gather_old(3, "vector", halves[1])
-        for part in halves:
-            subtract(3, part)
-        finish(1, [whole])
-        gather_adv(3, "scalar", whole)
-        for part in halves:
-            exponential(3, part, diff[3, part.start][:])
-        make_cap(3, whole)
-        finish(2, [whole])
-        for part in halves:
-            multiply(3, part)
-        finish(3, halves)
+            minimum(last, result, part)
+            nc.sync.dma_start(out_rows[:, last, part], result[:, part])

@@ -22,7 +22,6 @@ TILES = N // P
 PAIR = 2
 LOW, HIGH = 0.8, 1.25
 TABLE = 4 * U
-NEAR = 128
 
 
 def tile_picked_ppo8_none_p_kernel(tc, x_words, x_scales, w1, old, adv, offs, st, out):
@@ -42,9 +41,8 @@ def tile_picked_ppo8_none_p_kernel(tc, x_words, x_scales, w1, old, adv, offs, st
         for t in range(TILES):
             place[f"diff{t}_256"] = place[f"old{t}"]
             place[f"picked_old{t}"] = place[f"ratio{t}"] = (6 + t) * TABLE
-            place[f"plain{t}_{NEAR}"] = 10 * TABLE
             if t:
-                place[f"plain{t - 1}_0"] = place[f"old{t}"] + TABLE // 4
+                place[f"plain{t - 1}_0"] = 10 * TABLE
                 place[f"result{t - 1}"] = place[f"old{t}"] + TABLE // 2
 
         scale_table = shared.tile([P, T // 4], I32, name="scale_table", offset=place["scale_table"])
@@ -135,7 +133,6 @@ def tile_picked_ppo8_none_p_kernel(tc, x_words, x_scales, w1, old, adv, offs, st
             return keep.tile([P, width], F32, name=name)
 
         picked_old, a, diff, ratio, cap, plain = {}, {}, {}, {}, {}, {}
-        near, far = slice(0, NEAR), slice(NEAR, S)
 
         def gather_old(t):
             picked_old[t] = new(f"picked_old{t}")
@@ -173,12 +170,10 @@ def tile_picked_ppo8_none_p_kernel(tc, x_words, x_scales, w1, old, adv, offs, st
             gather_old(t)
             subtract(t)
             if t:
-                multiply(t - 1, near, nc.vector)
                 if t == 1:
                     adv_table[last] = load_table(adv_rows, last, f"adv{last}")
                 result = new(f"result{t - 1}")
-                for part in (far, near):
-                    minimum(t - 1, result, part)
+                minimum(t - 1, result, whole)
                 nc.sync.dma_start(out_rows[:, t - 1, :], result[:])
             gather_adv(t, [("scalar", whole)] if t else zip(("scalar", "vector"), halves))
             exponential(t)
@@ -186,7 +181,7 @@ def tile_picked_ppo8_none_p_kernel(tc, x_words, x_scales, w1, old, adv, offs, st
             if t == 0:
                 old_table[last] = load_table(old_rows, last, f"old{last}")
             if t < last:
-                multiply(t, far, nc.gpsimd)
+                multiply(t, whole, nc.gpsimd)
         for part in halves:
             multiply(last, part, nc.vector)
         result = new(f"result{last}")

@@ -21,6 +21,7 @@ QUADRANTS = 4
 TILES = N // P
 PAIR = 2
 LOW, HIGH = 0.8, 1.25
+CUT = S // 2 - 16
 TABLE = 4 * U
 
 
@@ -36,13 +37,11 @@ def tile_picked_ppo8_none_p_kernel(tc, x_words, x_scales, w1, old, adv, offs, st
             "scale_table": 3 * TABLE // 4, "old0": 0, "adv0": TABLE,
             "w_raw": 2 * TABLE, "old1": 2 * TABLE, "adv1": 3 * TABLE,
             "word_table": 4 * TABLE, "old2": 4 * TABLE, "adv2": 5 * TABLE,
-            "old3": 0, "adv3": 6 * TABLE,
+            "diff0_256": 0, "old3": 0, "adv3": 6 * TABLE, "plain0_0": 10 * TABLE, "plain1_0": 10 * TABLE,
         }
         for t in range(TILES):
-            place[f"diff{t}_256"] = place[f"old{t}"]
             place[f"picked_old{t}"] = place[f"ratio{t}"] = (6 + t) * TABLE
             if t:
-                place[f"plain{t - 1}_0"] = 10 * TABLE
                 place[f"result{t - 1}"] = place[f"old{t}"] + TABLE // 2
 
         scale_table = shared.tile([P, T // 4], I32, name="scale_table", offset=place["scale_table"])
@@ -134,29 +133,38 @@ def tile_picked_ppo8_none_p_kernel(tc, x_words, x_scales, w1, old, adv, offs, st
 
         picked_old, a, diff, ratio, cap, plain = {}, {}, {}, {}, {}, {}
 
-        def gather_old(t):
+        def gather_old(t, shares):
             picked_old[t] = new(f"picked_old{t}")
-            for engine, part in zip(("scalar", "vector"), halves):
+            for engine, part in shares:
                 gather(engine, picked_old[t][:, part], old_table[t], part)
 
         def subtract(t):
             for h, part in enumerate(halves):
-                diff[t, h] = new(f"diff{t}_{part.start}", S // 2)
-                nc.vector.tensor_tensor(diff[t, h][:], picked_old[t][:, part], y[t][h][:, part], ALU.subtract)
+                difference = new(f"diff{t}_{part.start}", S // 2)
+                nc.vector.tensor_tensor(difference[:], picked_old[t][:, part], y[t][h][:, part], ALU.subtract)
+                diff[t, part.start, part.stop] = difference[:]
+
+        def subtract_into_one(t, parts):
+            difference = new(f"diff{t}")
+            for part in parts:
+                nc.vector.tensor_tensor(difference[:, part], picked_old[t][:, part], y[t][0][:, part], ALU.subtract)
+            for part in (whole, *halves):
+                diff[t, part.start, part.stop] = difference[:, part]
 
         def gather_adv(t, shares):
             a[t] = new(f"a{t}")
             for engine, part in shares:
                 gather(engine, a[t][:, part], adv_table[t], part)
 
-        def exponential(t):
+        def exponential(t, parts):
             ratio[t] = new(f"ratio{t}")
-            for h, part in enumerate(halves):
-                nc.scalar.activation(ratio[t][:, part], diff[t, h][:], ACT.Exp, scale=-0.25)
+            for part in parts:
+                nc.scalar.activation(ratio[t][:, part], diff[t, part.start, part.stop], ACT.Exp, scale=-0.25)
 
-        def make_cap(t):
+        def make_cap(t, parts):
             cap[t] = new(f"cap{t}")
-            nc.vector.scalar_tensor_tensor(cap[t][:], a[t][:], HIGH / LOW, a[t][:], ALU.mult, ALU.max)
+            for part in parts:
+                nc.vector.scalar_tensor_tensor(cap[t][:, part], a[t][:, part], HIGH / LOW, a[t][:, part], ALU.mult, ALU.max)
 
         def multiply(t, part, engine):
             plain[t, part.start] = new(f"plain{t}_{part.start}", part.stop - part.start)
@@ -166,9 +174,17 @@ def tile_picked_ppo8_none_p_kernel(tc, x_words, x_scales, w1, old, adv, offs, st
             nc.vector.scalar_tensor_tensor(result[:, part], cap[t][:, part], LOW, plain[t, part.start][:], ALU.mult, ALU.min)
 
         last = TILES - 1
+        cut = [slice(0, CUT), slice(CUT, S)]
         for t in range(TILES):
-            gather_old(t)
-            subtract(t)
+            if t < last:
+                gather_old(t, zip(("scalar", "vector"), halves))
+                if t:
+                    subtract_into_one(t, cut)
+                else:
+                    subtract(t)
+            else:
+                gather_old(t, [("scalar", whole)])
+                subtract_into_one(t, [whole])
             if t:
                 if t == 1:
                     adv_table[last] = load_table(adv_rows, last, f"adv{last}")
@@ -176,12 +192,12 @@ def tile_picked_ppo8_none_p_kernel(tc, x_words, x_scales, w1, old, adv, offs, st
                 minimum(t - 1, result, whole)
                 nc.sync.dma_start(out_rows[:, t - 1, :], result[:])
             gather_adv(t, [("scalar", whole)] if t else zip(("scalar", "vector"), halves))
-            exponential(t)
-            make_cap(t)
+            exponential(t, [whole] if 0 < t < last else halves)
+            make_cap(t, [whole] if t else cut)
             if t == 0:
                 old_table[last] = load_table(old_rows, last, f"old{last}")
             if t < last:
-                multiply(t, whole, nc.gpsimd)
+                multiply(t, whole, nc.gpsimd if t < last - 1 else nc.vector)
         for part in halves:
             multiply(last, part, nc.vector)
         result = new(f"result{last}")

@@ -37,7 +37,7 @@ def tile_picked_ppo8_none_p_kernel(tc, x_words, x_scales, w1, old, adv, offs, st
             "scale_table": 3 * TABLE // 4, "old0": 0, "adv0": TABLE,
             "w_raw": 2 * TABLE, "old1": 2 * TABLE, "adv1": 3 * TABLE,
             "word_table": 4 * TABLE, "old2": 4 * TABLE, "adv2": 5 * TABLE,
-            "diff0_256": 0, "old3": 0, "adv3": 6 * TABLE, "plain0_0": 10 * TABLE, "plain1_0": 10 * TABLE,
+            "diff0_256": 0, "old3": 0, "adv3": 6 * TABLE, "plain0_0": 10 * TABLE, "plain1_0": 10 * TABLE, "plain2_0": 10 * TABLE,
         }
         for t in range(TILES):
             place[f"picked_old{t}"] = place[f"ratio{t}"] = (6 + t) * TABLE
@@ -176,15 +176,11 @@ def tile_picked_ppo8_none_p_kernel(tc, x_words, x_scales, w1, old, adv, offs, st
         last = TILES - 1
         cut = [slice(0, CUT), slice(CUT, S)]
         for t in range(TILES):
-            if t < last:
-                gather_old(t, zip(("scalar", "vector"), halves))
-                if t:
-                    subtract_into_one(t, cut)
-                else:
-                    subtract(t)
+            gather_old(t, zip(("scalar", "vector"), halves))
+            if t:
+                subtract_into_one(t, cut)
             else:
-                gather_old(t, [("scalar", whole)])
-                subtract_into_one(t, [whole])
+                subtract(t)
             if t:
                 if t == 1:
                     adv_table[last] = load_table(adv_rows, last, f"adv{last}")
@@ -197,7 +193,7 @@ def tile_picked_ppo8_none_p_kernel(tc, x_words, x_scales, w1, old, adv, offs, st
             if t == 0:
                 old_table[last] = load_table(old_rows, last, f"old{last}")
             if t < last:
-                multiply(t, whole, nc.gpsimd if t < last - 1 else nc.vector)
+                multiply(t, whole, nc.gpsimd)
         for part in halves:
             multiply(last, part, nc.vector)
         result = new(f"result{last}")

@@ -64,9 +64,9 @@ def tile_picked_ppo8_none_p_kernel(tc, x_words, x_scales, w1, old, adv, offs, st
         nc.sync.dma_start(offs_sb[:], offs)
         w_raw = shared.tile([P, PACK, N], F32, name="w_raw", offset=place["w_raw"])
         nc.sync.dma_start(w_raw[:], w1.rearrange("(p j) m -> p j m", j=PACK))
-        nc.sync.dma_start(st_sb[:], st)
         word_table = shared.tile([P, T], I32, name="word_table", offset=place["word_table"])
         nc.sync.dma_start(word_table[:], x_words[0].rearrange("p n r -> p (n r)").bitcast(I32))
+        nc.sync.dma_start(st_sb[:], st)
         picked_scales = keep.tile([P, S], U8, name="picked_scales")
         nc.vector.tensor_copy(picked_scales[:], scale_table[:].bitcast(U8).indirect(offs_sb[:]))
         for q in range(QUADRANTS):

from contextlib import ExitStack

import concourse.mybir as mybir

K, T, S, N, U = 512, 2048, 512, 512, 1024
FLOPS = 2 * K * N * S

F32 = mybir.dt.float32
BF16 = mybir.dt.bfloat16
I32 = mybir.dt.int32
U32 = mybir.dt.uint32
U16 = mybir.dt.uint16
U8 = mybir.dt.uint8
FP8X4 = mybir.dt.float8_e4m3fn_x4
ACT = mybir.ActivationFunctionType
ALU = mybir.AluOpType

P = 128
PACK = 4
QUADRANTS = 4
TILES = N // P
PAIR = 2
LOW, HIGH = 0.8, 1.25
CUT = S // 2 - 16
TABLE = 4 * U


def tile_picked_ppo8_none_p_kernel(tc, x_words, x_scales, w1, old, adv, offs, st, out):
    nc = tc.nc
    with ExitStack() as ctx:
        keep = ctx.enter_context(tc.tile_pool(name="keep", bufs=1))
        psum = ctx.enter_context(tc.psum_pool(name="psum", bufs=1))
        offs_sb = keep.tile([P, S // 16], U16, name="offs_sb")
        st_sb = keep.tile([P, S // 16], U16, name="st_sb")
        shared = ctx.enter_context(tc.tile_pool(name="shared", bufs=1))
        place = {
            "scale_table": 3 * TABLE // 4, "old0": 0, "adv0": TABLE,
            "w_raw": 2 * TABLE, "old1": 2 * TABLE, "adv1": 3 * TABLE,
            "word_table": 4 * TABLE, "old2": 4 * TABLE, "adv2": 5 * TABLE,
            "diff0_256": 0, "old3": 0, "adv3": 6 * TABLE, "plain0_0": 10 * TABLE, "plain1_0": 10 * TABLE, "plain2_0": 10 * TABLE,
        }
        for t in range(TILES):
            place[f"picked_old{t}"] = place[f"ratio{t}"] = (6 + t) * TABLE
            if t:
                place[f"result{t - 1}"] = place[f"old{t}"] + TABLE // 2

        scale_table = shared.tile([P, T // 4], I32, name="scale_table", offset=place["scale_table"])
        nc.gpsimd.memset(scale_table[:], 0)
        x_scale = keep.tile([P, S // 4], I32, name="x_scale", align_bytes=64)
        nc.gpsimd.memset(x_scale[:], 0)

        old_rows = old.rearrange("(p t) u -> p t u", t=TILES)
        adv_rows = adv.rearrange("(p t) u -> p t u", t=TILES)
        out_rows = out.rearrange("(p t) s -> p t s", t=TILES)

        def load_table(rows, t, name):
            table = shared.tile([P, U], F32, name=name, offset=place[name])
            nc.sync.dma_start(table[:], rows[:, t, :])
            return table

        scale_rows = keep.tile([16, T // 4], I32, name="scale_rows")
        nc.scalar.dma_start(scale_rows[:], x_scales[0].bitcast(I32))
        nc.vector.tensor_copy(scale_table[:16, :], scale_rows[:])
        nc.sync.dma_start(offs_sb[:], offs)
        w_raw = shared.tile([P, PACK, N], F32, name="w_raw", offset=place["w_raw"])
        nc.sync.dma_start(w_raw[:], w1.rearrange("(p j) m -> p j m", j=PACK))
        word_table = shared.tile([P, T], I32, name="word_table", offset=place["word_table"])
        nc.sync.dma_start(word_table[:], x_words[0].rearrange("p n r -> p (n r)").bitcast(I32))
        nc.sync.dma_start(st_sb[:], st)
        picked_scales = keep.tile([P, S], U8, name="picked_scales")
        nc.vector.tensor_copy(picked_scales[:], scale_table[:].bitcast(U8).indirect(offs_sb[:]))
        for q in range(QUADRANTS):
            nc.sync.dma_start(x_scale[32 * q : 32 * q + 4, :], picked_scales[4 * q : 4 * q + 4, :].bitcast(I32))

        w_code, w_scale = [], []
        blocks = [slice(b * P, (b + 1) * P) for b in range(S // P)]
        whole = slice(0, S)
        halves = [slice(0, S // 2), slice(S // 2, S)]

        def entries(lists, part):
            return lists[:, part.start // 16 : part.stop // 16]

        def quantize_weights(pair, cast):
            grouped = keep.tile([P, PAIR, P, PACK], BF16, name=f"grouped{pair}", align_bytes=64)
            columns = w_raw[:].rearrange("p j (c t) -> p c t j", t=TILES)[:, :, pair * PAIR : (pair + 1) * PAIR, :]
            cast(grouped[:].rearrange("p i c j -> p c i j"), columns)
            codes = keep.tile([P, PAIR * P], U32, name=f"w_code{pair}", align_bytes=64)
            scales = keep.tile([P, PAIR * P], U8, name=f"w_scale{pair}", align_bytes=64)
            nc.vector.quantize_mx(codes[:].bitcast(FP8X4), scales[:], grouped[:].rearrange("p i c j -> p (i c j)"))
            w_code.append(codes)
            w_scale.append(scales)

        def project(t, part, bank):
            pair, i = divmod(t, PAIR)
            y_ps = psum.tile([P, S], F32, name="y_ps", tag=f"bank{bank}")
            nc.tensor.matmul_mx(
                y_ps[:, part],
                lhsT=w_code[pair][:, blocks[i]].bitcast(FP8X4),
                lhsT_scale=w_scale[pair][:, blocks[i]],
                rhs=x_code[:, part].bitcast(FP8X4),
                rhs_scale=x_scale[:].bitcast(U8)[:, part],
                start=True,
                stop=True,
            )
            return y_ps

        def gather(engine, picked, table, part):
            looked_up = table[:].indirect(entries(st_sb, part))
            if engine == "scalar":
                nc.scalar.activation(picked, looked_up, ACT.Copy)
            else:
                nc.vector.tensor_copy(picked, looked_up)

        old_table = {0: load_table(old_rows, 0, "old0")}
        adv_table = {0: load_table(adv_rows, 0, "adv0")}
        quantize_weights(0, nc.vector.tensor_copy)
        quantize_weights(1, nc.scalar.copy)
        old_table[1] = load_table(old_rows, 1, "old1")
        adv_table[1] = load_table(adv_rows, 1, "adv1")
        x_code = keep.tile([P, S], U32, name="x_code", align_bytes=64)
        for part in halves:
            nc.vector.tensor_copy(x_code[:, part], word_table[:].bitcast(U32).indirect(entries(offs_sb, part)))
        old_table[2] = load_table(old_rows, 2, "old2")
        adv_table[2] = load_table(adv_rows, 2, "adv2")
        y = {0: [project(0, part, h) for h, part in enumerate(halves)]}
        for t in reversed(range(1, TILES)):
            y[t] = [project(t, whole, t + 1)] * 2

        def new(name, width=S):
            if name in place:
                return shared.tile([P, width], F32, name=name, offset=place[name])
            return keep.tile([P, width], F32, name=name)

        picked_old, a, diff, ratio, cap, plain = {}, {}, {}, {}, {}, {}

        def gather_old(t, shares):
            picked_old[t] = new(f"picked_old{t}")
            for engine, part in shares:
                gather(engine, picked_old[t][:, part], old_table[t], part)

        def subtract(t):
            for h, part in enumerate(halves):
                difference = new(f"diff{t}_{part.start}", S // 2)
                nc.vector.tensor_tensor(difference[:], picked_old[t][:, part], y[t][h][:, part], ALU.subtract)
                diff[t, part.start, part.stop] = difference[:]

        def subtract_into_one(t, parts):
            difference = new(f"diff{t}")
            for part in parts:
                nc.vector.tensor_tensor(difference[:, part], picked_old[t][:, part], y[t][0][:, part], ALU.subtract)
            for part in (whole, *halves):
                diff[t, part.start, part.stop] = difference[:, part]

        def gather_adv(t, shares):
            a[t] = new(f"a{t}")
            for engine, part in shares:
                gather(engine, a[t][:, part], adv_table[t], part)

        def exponential(t, parts):
            ratio[t] = new(f"ratio{t}")
            for part in parts:
                nc.scalar.activation(ratio[t][:, part], diff[t, part.start, part.stop], ACT.Exp, scale=-0.25)

        def make_cap(t, parts):
            cap[t] = new(f"cap{t}")
            for part in parts:
                nc.vector.scalar_tensor_tensor(cap[t][:, part], a[t][:, part], HIGH / LOW, a[t][:, part], ALU.mult, ALU.max)

        def multiply(t, part, engine):
            plain[t, part.start] = new(f"plain{t}_{part.start}", part.stop - part.start)
            engine.tensor_tensor(plain[t, part.start][:], ratio[t][:, part], a[t][:, part], ALU.mult)

        def minimum(t, result, part):
            nc.vector.scalar_tensor_tensor(result[:, part], cap[t][:, part], LOW, plain[t, part.start][:], ALU.mult, ALU.min)

        last = TILES - 1
        cut = [slice(0, CUT), slice(CUT, S)]
        for t in range(TILES):
            gather_old(t, zip(("scalar", "vector"), halves))
            if t:
                subtract_into_one(t, cut)
            else:
                subtract(t)
            if t:
                if t == 1:
                    adv_table[last] = load_table(adv_rows, last, f"adv{last}")
                result = new(f"result{t - 1}")
                minimum(t - 1, result, whole)
                nc.sync.dma_start(out_rows[:, t - 1, :], result[:])
            gather_adv(t, [("scalar", whole)] if t else zip(("scalar", "vector"), halves))
            exponential(t, [whole] if 0 < t < last else halves)
            make_cap(t, [whole] if t else cut)
            if t == 0:
                old_table[last] = load_table(old_rows, last, f"old{last}")
            if t < last:
                multiply(t, whole, nc.gpsimd)
        for part in halves:
            multiply(last, part, nc.vector)
        result = new(f"result{last}")
        for part in halves:
            minimum(last, result, part)
            nc.sync.dma_start(out_rows[:, last, part], result[:, part])
